import numpy as np
import ml_dtypes


def mxq(x, axis, fmt="e4m3"):
    dtype, down = {"e4m3": (ml_dtypes.float8_e4m3fn, 7), "e5m2": (ml_dtypes.float8_e5m2, 14)}[fmt]
    v = np.moveaxis(np.asarray(x, np.float32).astype(ml_dtypes.bfloat16).astype(np.float64), axis, -1)
    blocks = v.reshape(v.shape[:-1] + (-1, 32))
    amax = np.abs(blocks).max(-1, keepdims=True)
    byte = np.maximum(np.where(amax > 0, np.frexp(amax)[1] - 1 + 127, 0) - down, 1)
    scale = np.exp2(byte - 127.0)
    codes = (blocks / scale).astype(np.float32).astype(dtype).astype(np.float64)
    return np.moveaxis((codes * scale).reshape(v.shape), -1, axis)


WIDE = False


def mx_kscale(k):
    if not WIDE:
        return np.ones(k)
    levels = np.array([10, -10, 5, -5, 0])
    if k % 512:
        return np.exp2(np.random.permutation(np.resize(levels, k // 32))).repeat(32)
    a = np.empty((k // 512, 16))
    for p in range(k // 512):
        a[p, :8] = np.random.permutation(np.resize(levels, 8))
        for g in range(8):
            far = levels[np.abs(levels - a[p, g]) >= 10]
            a[p, g + 8] = far[np.random.randint(len(far))]
    return np.exp2(a.ravel()).repeat(32)


def f64(x):
    return np.asarray(x).astype(np.float64)


def striped(idx):
    return np.tile(idx.reshape(-1, 16).T, (8, 1)).astype(np.uint16)


def unstriped(offs):
    return offs[:16].T.reshape(-1).astype(np.int64)


E2M1 = np.array([0.0, 0.5, 1.0, 1.5, 2.0, 3.0, 4.0, 6.0, -0.0, -0.5, -1.0, -1.5, -2.0, -3.0, -4.0, -6.0])


def pack_weight(w, fmt):
    k, n = w.shape
    w = f64(np.asarray(w, np.float32).astype(ml_dtypes.bfloat16)).reshape(k // 32, 32, n)
    amax = np.abs(w).max(1)
    if fmt == "e4m3":
        byte = np.frexp(amax)[1] - 1 + 127 - 7
    else:
        mant, ex = np.frexp(amax / 6.0)
        byte = np.where(mant > 0.5, ex, ex - 1) + 127
    byte = np.clip(np.where(amax > 0, byte, 1), 1, 254)
    scaled = (w * np.exp2(127.0 - byte)[:, None, :]).reshape(k, n).astype(np.float32)
    by_word = np.ascontiguousarray(scaled.reshape(k // 512, 128, 4, n).transpose(0, 1, 3, 2))
    if fmt == "e4m3":
        words = by_word.astype(ml_dtypes.float8_e4m3fn).view(np.uint8)
    else:
        c = by_word.astype(ml_dtypes.float4_e2m1fn).view(np.uint8) & 0xF
        words = (c[..., 0::2] | (c[..., 1::2] << 4)).reshape(k // 512, 128, 2 * n)
    return np.ascontiguousarray(words), np.ascontiguousarray(byte.astype(np.uint8).reshape(k // 512, 16, n))


def unpack_weight(words, scales, fmt):
    g, _, n = scales.shape
    words = np.ascontiguousarray(words).reshape(g, 128, n, -1)
    if fmt == "e4m3":
        vals = words.view(ml_dtypes.float8_e4m3fn).astype(np.float64)
    else:
        nib = np.empty((g, 128, n, 4), np.uint8)
        nib[..., 0::2] = words & 0xF
        nib[..., 1::2] = words >> 4
        vals = E2M1[nib]
    vals = vals * np.repeat(np.exp2(scales.astype(np.float64) - 127.0), 8, axis=1)[..., None]
    return vals.transpose(0, 1, 3, 2).reshape(g * 512, n)


def gelu(v):
    return 0.5 * v * (1.0 + np.tanh(np.sqrt(2.0 / np.pi) * (v + 0.044715 * v**3)))


K, H, N, T, S, T2, P = 1536, 512, 384, 4096, 1024, 2048, 128

def setup_inputs():
    n = np.random.standard_normal
    s = mx_kscale(K)[:, None]
    u = mx_kscale(H)[:, None]
    tab_words, tab_scales = pack_weight(n((K, T)) * s, "e4m3")
    w2_words, w2_scales = pack_weight(n((K, H)) / np.sqrt(K) / s, "e2m1")
    return {
        "tab_words": tab_words, "tab_scales": tab_scales,
        "offs": striped(np.random.permutation(T)[:S]),
        "w1": (n((K, H)) / np.sqrt(K) / s * u.T).astype(np.float32),
        "w2_words": w2_words, "w2_scales": w2_scales,
        "w3": (1.5 * n((H, N)) / np.sqrt(H) / u).astype(np.float32),
        "by": (0.5 * n(N)).astype(np.float32),
        "wgo": np.exp(0.3 * n((P, S))).astype(np.float32),
        "offs2": striped(np.random.permutation(T2)[:S]),
    }

def reference(tab_words, tab_scales, offs, w1, w2_words, w2_scales, w3, by, wgo, offs2):
    v = unpack_weight(tab_words, tab_scales, "e4m3")[:, unstriped(offs)]
    w2 = unpack_weight(w2_words, w2_scales, "e2m1")
    a = mxq(f64(w1), 0, "e4m3").T @ v
    b = w2.T @ v
    h = a / (1.0 + np.abs(b))
    y = (mxq(f64(w3), 0, "e4m3").T @ mxq(h, 0, "e4m3")) + f64(by)[:, None]
    out = np.zeros((N, T2))
    out[:, unstriped(offs2)] = np.tile(f64(wgo), (N // P, 1)) * y
    return out

@@ -1,0 +1,244 @@
+from contextlib import ExitStack
+
+import concourse.mybir as mybir
+
+K, H, N, T, S, T2 = 1536, 512, 384, 4096, 1024, 2048
+P = 128
+PASSES = K // 512
+FLOPS = 2 * (2 * K * H * S + H * N * S)
+
+F32 = mybir.dt.float32
+BF16 = mybir.dt.bfloat16
+I32 = mybir.dt.int32
+U32 = mybir.dt.uint32
+U16 = mybir.dt.uint16
+U8 = mybir.dt.uint8
+FP8X4 = mybir.dt.float8_e4m3fn_x4
+FP4X4 = mybir.dt.float4_e2m1fn_x4
+ACT = mybir.ActivationFunctionType
+ALU = mybir.AluOpType
+
+CHUNK = 128
+HALF = 512
+SHIFT_ROWS = 100
+SC_BASE = 20
+GROUPS = ((0, 256), (256, 256), (512, 512))
+
+
+def tile_list_predicate_damped_store_kernel(
+    tc, tab_words, tab_scales, offs, w1, w2_words, w2_scales, w3, by, wgo, offs2, out
+):
+    nc = tc.nc
+    with ExitStack() as ctx:
+        keep = ctx.enter_context(tc.tile_pool(name="keep", bufs=1))
+        ring = ctx.enter_context(tc.tile_pool(name="ring", bufs=2))
+        big = ctx.enter_context(tc.tile_pool(name="big", bufs=3))
+        psum_ab = ctx.enter_context(tc.psum_pool(name="psum_ab", bufs=5))
+        psum_y = ctx.enter_context(tc.psum_pool(name="psum_y", bufs=3))
+
+        def held(shape, dtype, name):
+            return keep.tile(shape, dtype, name=name, align_bytes=64)
+
+        idx = keep.tile([P, S // 16], U16, name="idx")
+        idx2 = keep.tile([P, S // 16], U16, name="idx2")
+        tab = [big.tile([P, T], I32, name="tab%d" % a, tag="big", align_bytes=64) for a in range(PASSES)]
+        tab_sc = held([P, T // 4], I32, "tab_sc")
+        w2_raw = held([P, PASSES, H // 2], I32, "w2_raw")
+        w2_sc_raw = held([P, PASSES, H // 4], I32, "w2_sc_raw")
+        w1_first = held([P, 4, H], F32, "w1_first")
+        w1_rest = big.tile([P, PASSES - 1, 4, H], F32, name="w1_rest", tag="big", align_bytes=64)
+        w1_raw = [w1_first[:]] + [w1_rest[:, a] for a in range(PASSES - 1)]
+        w3_raw = big.tile([P, 4, N], F32, name="w3_raw", tag="big", align_bytes=64)
+        wgo_sb = big.tile([P, S], F32, name="wgo_sb", tag="big", align_bytes=64)
+        v_packed = held([P, S // 4], I32, "v_packed")
+        w2_codes = held([P, PASSES, H // 2], I32, "w2_codes")
+        w2_sc = held([P, PASSES, H // 4], I32, "w2_sc")
+        by_sb = held([P, N // P], F32, "by_sb")
+        v_sc = [held([P, S // 4], I32, "v_sc%d" % a) for a in range(PASSES)]
+        cache = [held([P, T2], F32, "cache%d" % n) for n in range(N // P)]
+        warm_in = held([P, 1], F32, "warm_in")
+        warm_out = held([P, 1], F32, "warm_out")
+
+        def load_w1(a):
+            nc.sync.dma_start(w1_raw[a], w1[512 * a : 512 * (a + 1), :].rearrange("(p j) c -> p j c", j=4))
+
+        for quad in range(4):
+            nc.scalar.dma_start(
+                tab_sc[32 * quad + SC_BASE : 32 * (quad + 1), :],
+                tab_scales[:, 4 * quad : 4 * quad + 4, :].bitcast(I32),
+            )
+        nc.sync.dma_start(idx[:], offs)
+        nc.sync.dma_start(idx2[:], offs2)
+        nc.sync.dma_start(w2_raw[:], w2_words.rearrange("a p b -> p a b").bitcast(I32))
+        load_w1(0)
+        for a in range(PASSES):
+            nc.sync.dma_start(tab[a][:], tab_words[a].rearrange("p t i -> p (t i)").bitcast(I32))
+        for quad in range(4):
+            nc.gpsimd.dma_start(
+                w2_sc_raw[32 * quad : 32 * quad + 4, :, :],
+                w2_scales[:, 4 * quad : 4 * quad + 4, :].rearrange("a r c -> r a c").bitcast(I32),
+            )
+        with nc.allow_non_contiguous_dma(reason="one bias value a partition"):
+            nc.gpsimd.dma_start(by_sb[:], by.rearrange("(n p) -> p n", p=P))
+
+        nc.vector.memset(warm_in[:], 1.0)
+        for quad in range(4):
+            nc.vector.memset(tab_sc[32 * quad : 32 * quad + SC_BASE, :], 0)
+        for a in range(PASSES):
+            nc.vector.memset(v_sc[a][96:P, :], 0)
+        nc.vector.memset(w2_sc[:], 0)
+        nc.scalar.activation(warm_out[:], warm_in[:], ACT.Abs_reciprocal_sqrt)
+
+        nc.vector.tensor_copy(v_packed[:].bitcast(U8), tab_sc[:].bitcast(U8).indirect(idx[:]))
+        for a in range(PASSES):
+            first_row = SC_BASE + 4 * a
+            nc.scalar.dma_start(v_sc[a][0:SHIFT_ROWS, :], v_packed[first_row : first_row + SHIFT_ROWS, :])
+
+        v_codes = {}
+        for a in range(PASSES):
+            for half in range(S // HALF):
+                gathered = held([P, HALF], I32, "v_codes%d_%d" % (a, half))
+                cols = slice(half * HALF // 16, (half + 1) * HALF // 16)
+                nc.vector.tensor_copy(gathered[:].bitcast(U32), tab[a][:].bitcast(U32).indirect(idx[:, cols]))
+                v_codes[a, half] = gathered
+
+        for a in range(1, PASSES):
+            load_w1(a)
+        w3_rows = w3.rearrange("(q t i) n -> t q i n", t=4, i=8)
+        for t in range(4):
+            nc.sync.dma_start(w3_raw[:, t, :], w3_rows[t])
+        nc.sync.dma_start(wgo_sb[:], wgo)
+
+        nc.vector.tensor_copy(
+            w2_codes[:].rearrange("p a (t q w) -> p a t q w", t=4, w=4),
+            w2_raw[:].rearrange("p a (q t w) -> p a t q w", t=4, w=4),
+        )
+        for quad in range(4):
+            rows = slice(32 * quad, 32 * quad + 4)
+            nc.vector.tensor_copy(
+                w2_sc[rows].rearrange("p a (t q w) -> p a t q w", t=4, w=2),
+                w2_sc_raw[rows].rearrange("p a (q t w) -> p a t q w", t=4, w=2),
+            )
+
+        def rhs(a, g):
+            half, start = divmod(g * CHUNK, HALF)
+            codes = v_codes[a, half][:, start : start + CHUNK].bitcast(FP8X4)
+            scales = v_sc[a][:].bitcast(U8)[:, g * CHUNK : (g + 1) * CHUNK]
+            return codes, scales
+
+        w1_codes = held([P, PASSES, H], U32, "w1_codes")
+        w1_sc = held([P, PASSES, H], U8, "w1_sc")
+        w1_bf = [held([P, H, 4], BF16, "w1_bf%d" % a) for a in range(PASSES)]
+        for a in range(PASSES):
+            src = w1_raw[a].rearrange("p j (q t i) -> p t q i j", t=4, i=8)
+            dst = w1_bf[a][:].rearrange("p (t q i) j -> p t q i j", t=4, i=8)
+            flat = w1_bf[a][:].rearrange("p m j -> p (m j)")
+            if a < PASSES - 1:
+                nc.vector.tensor_copy(dst, src)
+                nc.vector.quantize_mx(w1_codes[:, a, :].bitcast(FP8X4), w1_sc[:, a, :], flat)
+            else:
+                for t in range(4):
+                    nc.vector.tensor_copy(dst[:, t], src[:, t])
+                for t in range(4):
+                    cols = slice(P * t, P * (t + 1))
+                    nc.vector.quantize_mx(
+                        w1_codes[:, a, cols].bitcast(FP8X4), w1_sc[:, a, cols], flat[:, 512 * t : 512 * (t + 1)]
+                    )
+
+        w3_codes = held([P, N], U32, "w3_codes")
+        w3_sc = held([P, N], U8, "w3_sc")
+        w3_bf = held([P, N, 4], BF16, "w3_bf")
+        for n in range(N // P):
+            cols = slice(P * n, P * (n + 1))
+            nc.scalar.copy(w3_bf[:, cols, :], w3_raw[:, :, cols].rearrange("p t n -> p n t"))
+            nc.vector.quantize_mx(
+                w3_codes[:, cols].bitcast(FP8X4), w3_sc[:, cols], w3_bf[:, cols, :].rearrange("p n t -> p (n t)")
+            )
+
+        for n in range(N // P):
+            nc.vector.memset(cache[n][:], 0.0)
+
+        damp = {}
+
+        def damping(g):
+            b_ps = psum_ab.tile([P, 4, CHUNK], F32, name="b_ps", tag="ab")
+            for t in range(4):
+                for a in range(PASSES):
+                    codes, scales = rhs(a, g)
+                    nc.tensor.matmul_mx(
+                        b_ps[:, t, :],
+                        lhsT=w2_codes[:, a, 64 * t : 64 * (t + 1)].bitcast(U8).bitcast(FP4X4),
+                        lhsT_scale=w2_sc[:, a, 32 * t : 32 * (t + 1)].bitcast(U8),
+                        rhs=codes,
+                        rhs_scale=scales,
+                        start=(a == 0),
+                        stop=(a == PASSES - 1),
+                    )
+            b_abs = ring.tile([P, CHUNK, 4], F32, name="b_abs")
+            nc.scalar.activation(b_abs[:], b_ps[:].rearrange("p t n -> p n t"), ACT.Abs)
+            root = ring.tile([P, CHUNK, 4], F32, name="root")
+            nc.scalar.activation(root[:], b_abs[:], ACT.Abs_reciprocal_sqrt, bias=1.0)
+            factor = held([P, CHUNK, 4], F32, "damp%d" % g)
+            nc.scalar.activation(factor[:], root[:], ACT.Square)
+            damp[g] = factor
+
+        for g in range(4):
+            damping(g)
+
+        for first, count in GROUPS:
+            h_bf = held([P, count, 4], BF16, "h_bf%d" % first)
+            for g in range(first // CHUNK, (first + count) // CHUNK):
+                a_ps = psum_ab.tile([P, 4, CHUNK], F32, name="a_ps", tag="ab")
+                for t in range(4):
+                    cols = slice(P * t, P * (t + 1))
+                    for a in range(PASSES):
+                        codes, scales = rhs(a, g)
+                        nc.tensor.matmul_mx(
+                            a_ps[:, t, :],
+                            lhsT=w1_codes[:, a, cols].bitcast(FP8X4),
+                            lhsT_scale=w1_sc[:, a, cols],
+                            rhs=codes,
+                            rhs_scale=scales,
+                            start=(a == 0),
+                            stop=(a == PASSES - 1),
+                        )
+                start = g * CHUNK - first
+                nc.vector.tensor_tensor(
+                    h_bf[:, start : start + CHUNK, :], a_ps[:].rearrange("p t n -> p n t"), damp[g][:], ALU.mult
+                )
+            h_codes = held([P, count], U32, "h_codes%d" % first)
+            h_sc = held([P, count], U8, "h_sc%d" % first)
+            nc.vector.quantize_mx(h_codes[:].bitcast(FP8X4), h_sc[:], h_bf[:].rearrange("p n t -> p (n t)"))
+            y_sb = []
+
+            def project(n):
+                cols = slice(P * n, P * (n + 1))
+                y_ps = psum_y.tile([P, count], F32, name="y_ps")
+                nc.tensor.matmul_mx(
+                    y_ps[:],
+                    lhsT=w3_codes[:, cols].bitcast(FP8X4),
+                    lhsT_scale=w3_sc[:, cols],
+                    rhs=h_codes[:].bitcast(FP8X4),
+                    rhs_scale=h_sc[:],
+                    start=True,
+                    stop=True,
+                )
+                weighted = held([P, count], F32, "y_sb%d_%d" % (first, n))
+                nc.vector.scalar_tensor_tensor(
+                    weighted[:], y_ps[:], by_sb[:, n : n + 1], wgo_sb[:, first : first + count], ALU.add, ALU.mult
+                )
+                y_sb.append(weighted)
+
+            def place(n):
+                nc.vector.tensor_copy(cache[n][:].indirect(idx2[:, first // 16 : (first + count) // 16]), y_sb[n][:])
+                if first + count == S:
+                    nc.sync.dma_start(out[P * n : P * (n + 1), :], cache[n][:])
+
+            project(0)
+            project(1)
+            place(0)
+            project(2)
+            place(1)
+            place(2)
+            for g in range(len(damp), min(len(damp) + 2, S // CHUNK)):
+                damping(g)

@@ -32,7 +32,6 @@ def tile_list_predicate_damped_store_kernel(
     with ExitStack() as ctx:
         keep = ctx.enter_context(tc.tile_pool(name="keep", bufs=1))
         ring = ctx.enter_context(tc.tile_pool(name="ring", bufs=2))
-        big = ctx.enter_context(tc.tile_pool(name="big", bufs=3))
         psum_ab = ctx.enter_context(tc.psum_pool(name="psum_ab", bufs=5))
         psum_y = ctx.enter_context(tc.psum_pool(name="psum_y", bufs=3))
 
@@ -41,16 +40,15 @@ def tile_list_predicate_damped_store_kernel(
 
         idx = keep.tile([P, S // 16], U16, name="idx")
         idx2 = keep.tile([P, S // 16], U16, name="idx2")
-        tab = [big.tile([P, T], I32, name="tab%d" % a, tag="big", align_bytes=64) for a in range(PASSES)]
+        tab = [held([P, T], I32, "tab%d" % a) for a in range(PASSES)]
         tab_sc = held([P, T // 4], I32, "tab_sc")
         w2_raw = held([P, PASSES, H // 2], I32, "w2_raw")
         w2_sc_raw = held([P, PASSES, H // 4], I32, "w2_sc_raw")
-        w1_first = held([P, 4, H], F32, "w1_first")
-        w1_rest = big.tile([P, PASSES - 1, 4, H], F32, name="w1_rest", tag="big", align_bytes=64)
-        w1_raw = [w1_first[:]] + [w1_rest[:, a] for a in range(PASSES - 1)]
-        w3_raw = big.tile([P, 4, N], F32, name="w3_raw", tag="big", align_bytes=64)
-        wgo_sb = big.tile([P, S], F32, name="wgo_sb", tag="big", align_bytes=64)
+        w1_raw = [held([P, 4, H], F32, "w1_raw%d" % a) for a in range(PASSES - 1)]
+        w1_last = held([P, 2, 4, H // 2], F32, "w1_last")
         v_packed = held([P, S // 4], I32, "v_packed")
+        w3_raw = held([P, 4, N], F32, "w3_raw")
+        wgo_sb = held([P, S], F32, "wgo_sb")
         w2_codes = held([P, PASSES, H // 2], I32, "w2_codes")
         w2_sc = held([P, PASSES, H // 4], I32, "w2_sc")
         by_sb = held([P, N // P], F32, "by_sb")
@@ -59,48 +57,68 @@ def tile_list_predicate_damped_store_kernel(
         warm_in = held([P, 1], F32, "warm_in")
         warm_out = held([P, 1], F32, "warm_out")
 
-        def load_w1(a):
-            nc.sync.dma_start(w1_raw[a], w1[512 * a : 512 * (a + 1), :].rearrange("(p j) c -> p j c", j=4))
+        for quad in range(4):
+            nc.gpsimd.memset(tab_sc[32 * quad : 32 * quad + SC_BASE, :], 0)
+        for n in range(N // P):
+            nc.gpsimd.memset(cache[n][:], 0.0)
+        nc.vector.memset(warm_in[:], 1.0)
+        for a in range(PASSES):
+            nc.vector.memset(v_sc[a][96:P, :], 0)
+        nc.vector.memset(w2_sc[:], 0)
 
         for quad in range(4):
             nc.scalar.dma_start(
                 tab_sc[32 * quad + SC_BASE : 32 * (quad + 1), :],
                 tab_scales[:, 4 * quad : 4 * quad + 4, :].bitcast(I32),
             )
+        with nc.allow_non_contiguous_dma(reason="one bias value a partition"):
+            nc.scalar.dma_start(by_sb[:], by.rearrange("(n p) -> p n", p=P))
+        nc.scalar.activation(warm_out[:], warm_in[:], ACT.Abs_reciprocal_sqrt)
         nc.sync.dma_start(idx[:], offs)
-        nc.sync.dma_start(idx2[:], offs2)
         nc.sync.dma_start(w2_raw[:], w2_words.rearrange("a p b -> p a b").bitcast(I32))
+
+        def load_w1(a):
+            rows = w1[512 * a : 512 * (a + 1), :].rearrange("(p j) c -> p j c", j=4)
+            if a < PASSES - 1:
+                nc.sync.dma_start(w1_raw[a][:], rows)
+            else:
+                for u in range(2):
+                    nc.sync.dma_start(w1_last[:, u], rows[:, :, u * H // 2 : (u + 1) * H // 2])
+
+        nc.sync.dma_start(idx2[:], offs2)
         load_w1(0)
-        for a in range(PASSES):
+
+        def load_table(a):
             nc.sync.dma_start(tab[a][:], tab_words[a].rearrange("p t i -> p (t i)").bitcast(I32))
+
+        load_table(0)
         for quad in range(4):
-            nc.gpsimd.dma_start(
+            nc.sync.dma_start(
                 w2_sc_raw[32 * quad : 32 * quad + 4, :, :],
                 w2_scales[:, 4 * quad : 4 * quad + 4, :].rearrange("a r c -> r a c").bitcast(I32),
             )
-        with nc.allow_non_contiguous_dma(reason="one bias value a partition"):
-            nc.gpsimd.dma_start(by_sb[:], by.rearrange("(n p) -> p n", p=P))
-
-        nc.vector.memset(warm_in[:], 1.0)
-        for quad in range(4):
-            nc.vector.memset(tab_sc[32 * quad : 32 * quad + SC_BASE, :], 0)
-        for a in range(PASSES):
-            nc.vector.memset(v_sc[a][96:P, :], 0)
-        nc.vector.memset(w2_sc[:], 0)
-        nc.scalar.activation(warm_out[:], warm_in[:], ACT.Abs_reciprocal_sqrt)
+        load_table(1)
 
         nc.vector.tensor_copy(v_packed[:].bitcast(U8), tab_sc[:].bitcast(U8).indirect(idx[:]))
         for a in range(PASSES):
             first_row = SC_BASE + 4 * a
-            nc.scalar.dma_start(v_sc[a][0:SHIFT_ROWS, :], v_packed[first_row : first_row + SHIFT_ROWS, :])
+            nc.sync.dma_start(v_sc[a][0:SHIFT_ROWS, :], v_packed[first_row : first_row + SHIFT_ROWS, :])
+        load_table(2)
 
-        v_codes = {}
+        v_codes = []
+        v_halves = []
         for a in range(PASSES):
-            for half in range(S // HALF):
-                gathered = held([P, HALF], I32, "v_codes%d_%d" % (a, half))
-                cols = slice(half * HALF // 16, (half + 1) * HALF // 16)
+            width = HALF if a == PASSES - 1 else S
+            pieces = []
+            halves = []
+            for first in range(0, S, width):
+                gathered = held([P, width], I32, "v_codes%d_%d" % (a, first))
+                cols = slice(first // 16, (first + width) // 16)
                 nc.vector.tensor_copy(gathered[:].bitcast(U32), tab[a][:].bitcast(U32).indirect(idx[:, cols]))
-                v_codes[a, half] = gathered
+                pieces.extend(gathered[:, c : c + CHUNK] for c in range(0, width, CHUNK))
+                halves.extend(gathered[:, c : c + HALF] for c in range(0, width, HALF))
+            v_codes.append(pieces)
+            v_halves.append(halves)
 
         for a in range(1, PASSES):
             load_w1(a)
@@ -121,8 +139,7 @@ def tile_list_predicate_damped_store_kernel(
             )
 
         def rhs(a, g):
-            half, start = divmod(g * CHUNK, HALF)
-            codes = v_codes[a, half][:, start : start + CHUNK].bitcast(FP8X4)
+            codes = v_codes[a][g].bitcast(FP8X4)
             scales = v_sc[a][:].bitcast(U8)[:, g * CHUNK : (g + 1) * CHUNK]
             return codes, scales
 
@@ -130,15 +147,16 @@ def tile_list_predicate_damped_store_kernel(
         w1_sc = held([P, PASSES, H], U8, "w1_sc")
         w1_bf = [held([P, H, 4], BF16, "w1_bf%d" % a) for a in range(PASSES)]
         for a in range(PASSES):
-            src = w1_raw[a].rearrange("p j (q t i) -> p t q i j", t=4, i=8)
             dst = w1_bf[a][:].rearrange("p (t q i) j -> p t q i j", t=4, i=8)
             flat = w1_bf[a][:].rearrange("p m j -> p (m j)")
             if a < PASSES - 1:
-                nc.vector.tensor_copy(dst, src)
+                nc.vector.tensor_copy(dst, w1_raw[a][:].rearrange("p j (q t i) -> p t q i j", t=4, i=8))
                 nc.vector.quantize_mx(w1_codes[:, a, :].bitcast(FP8X4), w1_sc[:, a, :], flat)
             else:
-                for t in range(4):
-                    nc.vector.tensor_copy(dst[:, t], src[:, t])
+                for u in range(2):
+                    nc.vector.tensor_copy(
+                        dst[:, :, 8 * u : 8 * (u + 1)], w1_last[:, u].rearrange("p j (q t i) -> p t q i j", t=4, i=8)
+                    )
                 for t in range(4):
                     cols = slice(P * t, P * (t + 1))
                     nc.vector.quantize_mx(
@@ -150,95 +168,118 @@ def tile_list_predicate_damped_store_kernel(
         w3_bf = held([P, N, 4], BF16, "w3_bf")
         for n in range(N // P):
             cols = slice(P * n, P * (n + 1))
-            nc.scalar.copy(w3_bf[:, cols, :], w3_raw[:, :, cols].rearrange("p t n -> p n t"))
-            nc.vector.quantize_mx(
-                w3_codes[:, cols].bitcast(FP8X4), w3_sc[:, cols], w3_bf[:, cols, :].rearrange("p n t -> p (n t)")
+            nc.gpsimd.tensor_scalar(
+                w3_bf[:, cols, :], w3_raw[:, :, cols].rearrange("p t n -> p n t"), 1.0, 0.0, ALU.mult, ALU.add
             )
 
-        for n in range(N // P):
-            nc.vector.memset(cache[n][:], 0.0)
+        b_abs = [held([P, 4, HALF], F32, "b_abs%d" % half) for half in range(S // HALF)]
+        for half in range(S // HALF):
+            for t in range(4):
+                b_ps = psum_ab.tile([P, HALF], F32, name="b_ps", tag="ab")
+                for a in range(PASSES):
+                    nc.tensor.matmul_mx(
+                        b_ps[:],
+                        lhsT=w2_codes[:, a, 64 * t : 64 * (t + 1)].bitcast(U8).bitcast(FP4X4),
+                        lhsT_scale=w2_sc[:, a, 32 * t : 32 * (t + 1)].bitcast(U8),
+                        rhs=v_halves[a][half].bitcast(FP8X4),
+                        rhs_scale=v_sc[a][:].bitcast(U8)[:, half * HALF : (half + 1) * HALF],
+                        start=(a == 0),
+                        stop=(a == PASSES - 1),
+                    )
+                nc.scalar.activation(b_abs[half][:, t, :], b_ps[:], ACT.Abs)
 
-        damp = {}
+        damp = []
+        for g in range(S // CHUNK):
+            damp.append(held([P, CHUNK, 4], F32, "damp%d" % g))
 
         def damping(g):
-            b_ps = psum_ab.tile([P, 4, CHUNK], F32, name="b_ps", tag="ab")
+            half, start = divmod(g * CHUNK, HALF)
+            root = ring.tile([P, CHUNK, 4], F32, name="root")
+            nc.scalar.activation(
+                root[:],
+                b_abs[half][:, :, start : start + CHUNK].rearrange("p t n -> p n t"),
+                ACT.Abs_reciprocal_sqrt,
+                bias=1.0,
+            )
+            nc.scalar.activation(damp[g][:], root[:], ACT.Square)
+
+        h_bf = [held([P, count, 4], BF16, "h_bf%d" % first) for first, count in GROUPS]
+        h_codes = [held([P, count], U32, "h_codes%d" % first) for first, count in GROUPS]
+        h_sc = [held([P, count], U8, "h_sc%d" % first) for first, count in GROUPS]
+
+        def signal(g):
+            group = max(k for k in range(len(GROUPS)) if GROUPS[k][0] <= g * CHUNK)
+            first, count = GROUPS[group]
+            a_ps = psum_ab.tile([P, 4, CHUNK], F32, name="a_ps", tag="ab")
             for t in range(4):
+                cols = slice(P * t, P * (t + 1))
                 for a in range(PASSES):
                     codes, scales = rhs(a, g)
                     nc.tensor.matmul_mx(
-                        b_ps[:, t, :],
-                        lhsT=w2_codes[:, a, 64 * t : 64 * (t + 1)].bitcast(U8).bitcast(FP4X4),
-                        lhsT_scale=w2_sc[:, a, 32 * t : 32 * (t + 1)].bitcast(U8),
+                        a_ps[:, t, :],
+                        lhsT=w1_codes[:, a, cols].bitcast(FP8X4),
+                        lhsT_scale=w1_sc[:, a, cols],
                         rhs=codes,
                         rhs_scale=scales,
                         start=(a == 0),
                         stop=(a == PASSES - 1),
                     )
-            b_abs = ring.tile([P, CHUNK, 4], F32, name="b_abs")
-            nc.scalar.activation(b_abs[:], b_ps[:].rearrange("p t n -> p n t"), ACT.Abs)
-            root = ring.tile([P, CHUNK, 4], F32, name="root")
-            nc.scalar.activation(root[:], b_abs[:], ACT.Abs_reciprocal_sqrt, bias=1.0)
-            factor = held([P, CHUNK, 4], F32, "damp%d" % g)
-            nc.scalar.activation(factor[:], root[:], ACT.Square)
-            damp[g] = factor
+            start = g * CHUNK - first
+            nc.vector.tensor_tensor(
+                h_bf[group][:, start : start + CHUNK, :], a_ps[:].rearrange("p t n -> p n t"), damp[g][:], ALU.mult
+            )
+            if start + CHUNK == count:
+                nc.vector.quantize_mx(
+                    h_codes[group][:].bitcast(FP8X4), h_sc[group][:], h_bf[group][:].rearrange("p n t -> p (n t)")
+                )
+
+        def project(group, n):
+            first, count = GROUPS[group]
+            cols = slice(P * n, P * (n + 1))
+            if group == 0:
+                nc.vector.quantize_mx(
+                    w3_codes[:, cols].bitcast(FP8X4), w3_sc[:, cols], w3_bf[:, cols, :].rearrange("p n t -> p (n t)")
+                )
+            y_ps = psum_y.tile([P, count], F32, name="y_ps")
+            nc.tensor.matmul_mx(
+                y_ps[:],
+                lhsT=w3_codes[:, cols].bitcast(FP8X4),
+                lhsT_scale=w3_sc[:, cols],
+                rhs=h_codes[group][:].bitcast(FP8X4),
+                rhs_scale=h_sc[group][:],
+                start=True,
+                stop=True,
+            )
+            y_sb = held([P, count], F32, "y_sb%d_%d" % (group, n))
+            nc.scalar.activation(y_sb[:], y_ps[:], ACT.Identity, bias=by_sb[:, n : n + 1])
+            nc.vector.tensor_tensor(
+                cache[n][:].indirect(idx2[:, first // 16 : (first + count) // 16]),
+                y_sb[:],
+                wgo_sb[:, first : first + count],
+                ALU.mult,
+            )
+            if first + count == S:
+                nc.sync.dma_start(out[cols, :], cache[n][:])
 
         for g in range(4):
             damping(g)
-
-        for first, count in GROUPS:
-            h_bf = held([P, count, 4], BF16, "h_bf%d" % first)
-            for g in range(first // CHUNK, (first + count) // CHUNK):
-                a_ps = psum_ab.tile([P, 4, CHUNK], F32, name="a_ps", tag="ab")
-                for t in range(4):
-                    cols = slice(P * t, P * (t + 1))
-                    for a in range(PASSES):
-                        codes, scales = rhs(a, g)
-                        nc.tensor.matmul_mx(
-                            a_ps[:, t, :],
-                            lhsT=w1_codes[:, a, cols].bitcast(FP8X4),
-                            lhsT_scale=w1_sc[:, a, cols],
-                            rhs=codes,
-                            rhs_scale=scales,
-                            start=(a == 0),
-                            stop=(a == PASSES - 1),
-                        )
-                start = g * CHUNK - first
-                nc.vector.tensor_tensor(
-                    h_bf[:, start : start + CHUNK, :], a_ps[:].rearrange("p t n -> p n t"), damp[g][:], ALU.mult
-                )
-            h_codes = held([P, count], U32, "h_codes%d" % first)
-            h_sc = held([P, count], U8, "h_sc%d" % first)
-            nc.vector.quantize_mx(h_codes[:].bitcast(FP8X4), h_sc[:], h_bf[:].rearrange("p n t -> p (n t)"))
-            y_sb = []
-
-            def project(n):
-                cols = slice(P * n, P * (n + 1))
-                y_ps = psum_y.tile([P, count], F32, name="y_ps")
-                nc.tensor.matmul_mx(
-                    y_ps[:],
-                    lhsT=w3_codes[:, cols].bitcast(FP8X4),
-                    lhsT_scale=w3_sc[:, cols],
-                    rhs=h_codes[:].bitcast(FP8X4),
-                    rhs_scale=h_sc[:],
-                    start=True,
-                    stop=True,
-                )
-                weighted = held([P, count], F32, "y_sb%d_%d" % (first, n))
-                nc.vector.scalar_tensor_tensor(
-                    weighted[:], y_ps[:], by_sb[:, n : n + 1], wgo_sb[:, first : first + count], ALU.add, ALU.mult
-                )
-                y_sb.append(weighted)
-
-            def place(n):
-                nc.vector.tensor_copy(cache[n][:].indirect(idx2[:, first // 16 : (first + count) // 16]), y_sb[n][:])
-                if first + count == S:
-                    nc.sync.dma_start(out[P * n : P * (n + 1), :], cache[n][:])
-
-            project(0)
-            project(1)
-            place(0)
-            project(2)
-            place(1)
-            place(2)
-            for g in range(len(damp), min(len(damp) + 2, S // CHUNK)):
-                damping(g)
+        signal(0)
+        signal(1)
+        signal(2)
+        project(0, 0)
+        damping(4)
+        signal(3)
+        project(0, 1)
+        project(0, 2)
+        damping(5)
+        signal(4)
+        project(1, 0)
+        damping(6)
+        signal(5)
+        damping(7)
+        signal(6)
+        project(1, 1)
+        signal(7)
+        project(1, 2)
+        for n in range(N // P):
+            project(2, n)

@@ -22,6 +22,8 @@ CHUNK = 128
 HALF = 512
 SHIFT_ROWS = 100
 SC_BASE = 20
+A_BANKS = (0, 1, 2, 3, 6, 7, 1, 4)
+Y_BANKS = ((4, 5, 3), (0, 2, 4), (5, 0, 6))
 GROUPS = ((0, 256), (256, 256), (512, 512))
 
 
@@ -32,8 +34,7 @@ def tile_list_predicate_damped_store_kernel(
     with ExitStack() as ctx:
         keep = ctx.enter_context(tc.tile_pool(name="keep", bufs=1))
         ring = ctx.enter_context(tc.tile_pool(name="ring", bufs=2))
-        psum_ab = ctx.enter_context(tc.psum_pool(name="psum_ab", bufs=5))
-        psum_y = ctx.enter_context(tc.psum_pool(name="psum_y", bufs=3))
+        psum = ctx.enter_context(tc.psum_pool(name="psum", bufs=1))
 
         def held(shape, dtype, name):
             return keep.tile(shape, dtype, name=name, align_bytes=64)
@@ -58,6 +59,12 @@ def tile_list_predicate_damped_store_kernel(
         warm_out = held([P, 1], F32, "warm_out")
 
         for quad in range(4):
+            nc.gpsimd.dma_start(
+                tab_sc[32 * quad + SC_BASE : 32 * (quad + 1), :],
+                tab_scales[:, 4 * quad : 4 * quad + 4, :].bitcast(I32),
+            )
+
+        for quad in range(4):
             nc.gpsimd.memset(tab_sc[32 * quad : 32 * quad + SC_BASE, :], 0)
         for n in range(N // P):
             nc.gpsimd.memset(cache[n][:], 0.0)
@@ -66,11 +73,6 @@ def tile_list_predicate_damped_store_kernel(
             nc.vector.memset(v_sc[a][96:P, :], 0)
         nc.vector.memset(w2_sc[:], 0)
 
-        for quad in range(4):
-            nc.scalar.dma_start(
-                tab_sc[32 * quad + SC_BASE : 32 * (quad + 1), :],
-                tab_scales[:, 4 * quad : 4 * quad + 4, :].bitcast(I32),
-            )
         with nc.allow_non_contiguous_dma(reason="one bias value a partition"):
             nc.scalar.dma_start(by_sb[:], by.rearrange("(n p) -> p n", p=P))
         nc.scalar.activation(warm_out[:], warm_in[:], ACT.Abs_reciprocal_sqrt)
@@ -166,16 +168,11 @@ def tile_list_predicate_damped_store_kernel(
         w3_codes = held([P, N], U32, "w3_codes")
         w3_sc = held([P, N], U8, "w3_sc")
         w3_bf = held([P, N, 4], BF16, "w3_bf")
-        for n in range(N // P):
-            cols = slice(P * n, P * (n + 1))
-            nc.gpsimd.tensor_scalar(
-                w3_bf[:, cols, :], w3_raw[:, :, cols].rearrange("p t n -> p n t"), 1.0, 0.0, ALU.mult, ALU.add
-            )
 
         b_abs = [held([P, 4, HALF], F32, "b_abs%d" % half) for half in range(S // HALF)]
         for half in range(S // HALF):
             for t in range(4):
-                b_ps = psum_ab.tile([P, HALF], F32, name="b_ps", tag="ab")
+                b_ps = psum.tile([P, HALF], F32, name="b_ps", tag="bank%d" % (4 * half + t))
                 for a in range(PASSES):
                     nc.tensor.matmul_mx(
                         b_ps[:],
@@ -210,7 +207,7 @@ def tile_list_predicate_damped_store_kernel(
         def signal(g):
             group = max(k for k in range(len(GROUPS)) if GROUPS[k][0] <= g * CHUNK)
             first, count = GROUPS[group]
-            a_ps = psum_ab.tile([P, 4, CHUNK], F32, name="a_ps", tag="ab")
+            a_ps = psum.tile([P, 4, CHUNK], F32, name="a_ps", tag="bank%d" % A_BANKS[g])
             for t in range(4):
                 cols = slice(P * t, P * (t + 1))
                 for a in range(PASSES):
@@ -237,10 +234,11 @@ def tile_list_predicate_damped_store_kernel(
             first, count = GROUPS[group]
             cols = slice(P * n, P * (n + 1))
             if group == 0:
+                nc.vector.tensor_copy(w3_bf[:, cols, :], w3_raw[:, :, cols].rearrange("p t n -> p n t"))
                 nc.vector.quantize_mx(
                     w3_codes[:, cols].bitcast(FP8X4), w3_sc[:, cols], w3_bf[:, cols, :].rearrange("p n t -> p (n t)")
                 )
-            y_ps = psum_y.tile([P, count], F32, name="y_ps")
+            y_ps = psum.tile([P, count], F32, name="y_ps", tag="bank%d" % Y_BANKS[group][n])
             nc.tensor.matmul_mx(
                 y_ps[:],
                 lhsT=w3_codes[:, cols].bitcast(FP8X4),

@@ -20,10 +20,10 @@ ALU = mybir.AluOpType
 
 CHUNK = 128
 HALF = 512
-SHIFT_ROWS = 100
-SC_BASE = 20
-A_BANKS = (0, 1, 2, 3, 6, 7, 1, 4)
-Y_BANKS = ((4, 5, 3), (0, 2, 4), (5, 0, 6))
+SC_BASE = (0, 4, 1)
+MOVES_BEFORE_TABLE = {3: 1, 9: 2}
+A_BANKS = (4, 5, 6, 7, 6, 0, 1, 2)
+Y_BANKS = ((4, 5, 7), (3, 4, 2), (5, 6, 0))
 GROUPS = ((0, 256), (256, 256), (512, 512))
 
 
@@ -45,8 +45,11 @@ def tile_list_predicate_damped_store_kernel(
         tab_sc = held([P, T // 4], I32, "tab_sc")
         w2_raw = held([P, PASSES, H // 2], I32, "w2_raw")
         w2_sc_raw = held([P, PASSES, H // 4], I32, "w2_sc_raw")
-        w1_raw = [held([P, 4, H], F32, "w1_raw%d" % a) for a in range(PASSES - 1)]
-        w1_last = held([P, 2, 4, H // 2], F32, "w1_last")
+        w1_first = held([P, 4, H], F32, "w1_first")
+        w1_raw = {}
+        for a in range(1, PASSES):
+            for u in range(2):
+                w1_raw[a, u] = held([P, 4, H // 2], F32, "w1_raw%d_%d" % (a, u))
         v_packed = held([P, S // 4], I32, "v_packed")
         w3_raw = held([P, 4, N], F32, "w3_raw")
         wgo_sb = held([P, S], F32, "wgo_sb")
@@ -54,73 +57,62 @@ def tile_list_predicate_damped_store_kernel(
         w2_sc = held([P, PASSES, H // 4], I32, "w2_sc")
         by_sb = held([P, N // P], F32, "by_sb")
         v_sc = [held([P, S // 4], I32, "v_sc%d" % a) for a in range(PASSES)]
-        cache = [held([P, T2], F32, "cache%d" % n) for n in range(N // P)]
         warm_in = held([P, 1], F32, "warm_in")
         warm_out = held([P, 1], F32, "warm_out")
 
-        for quad in range(4):
-            nc.gpsimd.dma_start(
-                tab_sc[32 * quad + SC_BASE : 32 * (quad + 1), :],
-                tab_scales[:, 4 * quad : 4 * quad + 4, :].bitcast(I32),
-            )
-
-        for quad in range(4):
-            nc.gpsimd.memset(tab_sc[32 * quad : 32 * quad + SC_BASE, :], 0)
-        for n in range(N // P):
-            nc.gpsimd.memset(cache[n][:], 0.0)
-        nc.vector.memset(warm_in[:], 1.0)
+        nc.gpsimd.memset(tab_sc[:], 0)
         for a in range(PASSES):
-            nc.vector.memset(v_sc[a][96:P, :], 0)
-        nc.vector.memset(w2_sc[:], 0)
-
-        with nc.allow_non_contiguous_dma(reason="one bias value a partition"):
-            nc.scalar.dma_start(by_sb[:], by.rearrange("(n p) -> p n", p=P))
+            nc.gpsimd.memset(v_sc[a][:], 0)
+        nc.gpsimd.memset(w2_sc[:], 0)
+        nc.vector.memset(warm_in[:], 1.0)
         nc.scalar.activation(warm_out[:], warm_in[:], ACT.Abs_reciprocal_sqrt)
-        nc.sync.dma_start(idx[:], offs)
-        nc.sync.dma_start(w2_raw[:], w2_words.rearrange("a p b -> p a b").bitcast(I32))
 
         def load_w1(a):
             rows = w1[512 * a : 512 * (a + 1), :].rearrange("(p j) c -> p j c", j=4)
-            if a < PASSES - 1:
-                nc.sync.dma_start(w1_raw[a][:], rows)
+            if a == 0:
+                nc.sync.dma_start(w1_first[:], rows)
             else:
                 for u in range(2):
-                    nc.sync.dma_start(w1_last[:, u], rows[:, :, u * H // 2 : (u + 1) * H // 2])
-
-        nc.sync.dma_start(idx2[:], offs2)
-        load_w1(0)
+                    nc.sync.dma_start(w1_raw[a, u][:], rows[:, :, u * H // 2 : (u + 1) * H // 2])
 
         def load_table(a):
             nc.sync.dma_start(tab[a][:], tab_words[a].rearrange("p t i -> p (t i)").bitcast(I32))
 
-        load_table(0)
-        for quad in range(4):
+        def load_w2_scales(quad):
             nc.sync.dma_start(
                 w2_sc_raw[32 * quad : 32 * quad + 4, :, :],
                 w2_scales[:, 4 * quad : 4 * quad + 4, :].rearrange("a r c -> r a c").bitcast(I32),
             )
-        load_table(1)
+
+        nc.sync.dma_start(idx[:], offs)
+        nc.sync.dma_start(w2_raw[:], w2_words.rearrange("a p b -> p a b").bitcast(I32))
+        for a in range(PASSES):
+            nc.sync.dma_start(tab_sc[SC_BASE[a] : P : 8, :], tab_scales[a].bitcast(I32))
+        load_w2_scales(0)
+        load_w1(0)
+        load_table(0)
+        for quad in range(1, 4):
+            load_w2_scales(quad)
 
         nc.vector.tensor_copy(v_packed[:].bitcast(U8), tab_sc[:].bitcast(U8).indirect(idx[:]))
-        for a in range(PASSES):
-            first_row = SC_BASE + 4 * a
-            nc.sync.dma_start(v_sc[a][0:SHIFT_ROWS, :], v_packed[first_row : first_row + SHIFT_ROWS, :])
-        load_table(2)
+        moves = [(a, r) for a in range(PASSES) for r in range(4)]
+        for k, (a, r) in enumerate(moves):
+            if k in MOVES_BEFORE_TABLE:
+                load_table(MOVES_BEFORE_TABLE[k])
+            nc.sync.dma_start(v_sc[a][r:P:32, :], v_packed[SC_BASE[a] + 8 * r : P : 32, :])
 
-        v_codes = []
-        v_halves = []
-        for a in range(PASSES):
-            width = HALF if a == PASSES - 1 else S
-            pieces = []
-            halves = []
-            for first in range(0, S, width):
-                gathered = held([P, width], I32, "v_codes%d_%d" % (a, first))
-                cols = slice(first // 16, (first + width) // 16)
-                nc.vector.tensor_copy(gathered[:].bitcast(U32), tab[a][:].bitcast(U32).indirect(idx[:, cols]))
-                pieces.extend(gathered[:, c : c + CHUNK] for c in range(0, width, CHUNK))
-                halves.extend(gathered[:, c : c + HALF] for c in range(0, width, HALF))
-            v_codes.append(pieces)
-            v_halves.append(halves)
+        v_halves = {}
+
+        def gather_words(a, first, width, tag):
+            gathered = keep.tile([P, width], I32, name="v_codes", tag=tag, align_bytes=64)
+            cols = slice(first // 16, (first + width) // 16)
+            nc.vector.tensor_copy(gathered[:].bitcast(U32), tab[a][:].bitcast(U32).indirect(idx[:, cols]))
+            for c in range(0, width, HALF):
+                v_halves[a, (first + c) // HALF] = gathered[:, c : c + HALF]
+
+        gather_words(0, 0, S, "v_codes0")
+        gather_words(1, 0, S, "v_codes1")
+        gather_words(2, 0, HALF, "v_codes2")
 
         for a in range(1, PASSES):
             load_w1(a)
@@ -128,6 +120,9 @@ def tile_list_predicate_damped_store_kernel(
         for t in range(4):
             nc.sync.dma_start(w3_raw[:, t, :], w3_rows[t])
         nc.sync.dma_start(wgo_sb[:], wgo)
+        nc.sync.dma_start(idx2[:], offs2)
+        with nc.allow_non_contiguous_dma(reason="one bias value a partition"):
+            nc.sync.dma_start(by_sb[:], by.rearrange("(n p) -> p n", p=P))
 
         nc.vector.tensor_copy(
             w2_codes[:].rearrange("p a (t q w) -> p a t q w", t=4, w=4),
@@ -141,7 +136,8 @@ def tile_list_predicate_damped_store_kernel(
             )
 
         def rhs(a, g):
-            codes = v_codes[a][g].bitcast(FP8X4)
+            half, start = divmod(g * CHUNK, HALF)
+            codes = v_halves[a, half][:, start : start + CHUNK].bitcast(FP8X4)
             scales = v_sc[a][:].bitcast(U8)[:, g * CHUNK : (g + 1) * CHUNK]
             return codes, scales
 
@@ -151,34 +147,44 @@ def tile_list_predicate_damped_store_kernel(
         for a in range(PASSES):
             dst = w1_bf[a][:].rearrange("p (t q i) j -> p t q i j", t=4, i=8)
             flat = w1_bf[a][:].rearrange("p m j -> p (m j)")
-            if a < PASSES - 1:
-                nc.vector.tensor_copy(dst, w1_raw[a][:].rearrange("p j (q t i) -> p t q i j", t=4, i=8))
-                nc.vector.quantize_mx(w1_codes[:, a, :].bitcast(FP8X4), w1_sc[:, a, :], flat)
+            if a == 0:
+                nc.vector.tensor_copy(dst, w1_first[:].rearrange("p j (q t i) -> p t q i j", t=4, i=8))
             else:
                 for u in range(2):
                     nc.vector.tensor_copy(
-                        dst[:, :, 8 * u : 8 * (u + 1)], w1_last[:, u].rearrange("p j (q t i) -> p t q i j", t=4, i=8)
+                        dst[:, :, 8 * u : 8 * (u + 1)], w1_raw[a, u][:].rearrange("p j (q t i) -> p t q i j", t=4, i=8)
                     )
+            if a < PASSES - 1:
+                nc.vector.quantize_mx(w1_codes[:, a, :].bitcast(FP8X4), w1_sc[:, a, :], flat)
+            else:
                 for t in range(4):
                     cols = slice(P * t, P * (t + 1))
                     nc.vector.quantize_mx(
                         w1_codes[:, a, cols].bitcast(FP8X4), w1_sc[:, a, cols], flat[:, 512 * t : 512 * (t + 1)]
                     )
+        gather_words(2, HALF, HALF, "w1_raw2_1")
+
+        cache = []
+        for tag in ("tab_sc", "w1_first", "tab0"):
+            zeroed = keep.tile([P, T2], F32, name="cache", tag=tag, align_bytes=64)
+            nc.gpsimd.memset(zeroed[:], 0.0)
+            cache.append(zeroed)
 
         w3_codes = held([P, N], U32, "w3_codes")
         w3_sc = held([P, N], U8, "w3_sc")
         w3_bf = held([P, N, 4], BF16, "w3_bf")
 
         b_abs = [held([P, 4, HALF], F32, "b_abs%d" % half) for half in range(S // HALF)]
-        for half in range(S // HALF):
+
+        def load_half(half):
             for t in range(4):
-                b_ps = psum.tile([P, HALF], F32, name="b_ps", tag="bank%d" % (4 * half + t))
+                b_ps = psum.tile([P, HALF], F32, name="b_ps", tag="bank%d" % t)
                 for a in range(PASSES):
                     nc.tensor.matmul_mx(
                         b_ps[:],
                         lhsT=w2_codes[:, a, 64 * t : 64 * (t + 1)].bitcast(U8).bitcast(FP4X4),
                         lhsT_scale=w2_sc[:, a, 32 * t : 32 * (t + 1)].bitcast(U8),
-                        rhs=v_halves[a][half].bitcast(FP8X4),
+                        rhs=v_halves[a, half].bitcast(FP8X4),
                         rhs_scale=v_sc[a][:].bitcast(U8)[:, half * HALF : (half + 1) * HALF],
                         start=(a == 0),
                         stop=(a == PASSES - 1),
@@ -196,7 +202,7 @@ def tile_list_predicate_damped_store_kernel(
                 root[:],
                 b_abs[half][:, :, start : start + CHUNK].rearrange("p t n -> p n t"),
                 ACT.Abs_reciprocal_sqrt,
-                bias=1.0,
+                bias=warm_out[:],
             )
             nc.scalar.activation(damp[g][:], root[:], ACT.Square)
 
@@ -234,7 +240,6 @@ def tile_list_predicate_damped_store_kernel(
             first, count = GROUPS[group]
             cols = slice(P * n, P * (n + 1))
             if group == 0:
-                nc.vector.tensor_copy(w3_bf[:, cols, :], w3_raw[:, :, cols].rearrange("p t n -> p n t"))
                 nc.vector.quantize_mx(
                     w3_codes[:, cols].bitcast(FP8X4), w3_sc[:, cols], w3_bf[:, cols, :].rearrange("p n t -> p (n t)")
                 )
@@ -259,16 +264,27 @@ def tile_list_predicate_damped_store_kernel(
             if first + count == S:
                 nc.sync.dma_start(out[cols, :], cache[n][:])
 
-        for g in range(4):
-            damping(g)
+        def round_w3(n):
+            cols = slice(P * n, P * (n + 1))
+            nc.scalar.copy(w3_bf[:, cols, :], w3_raw[:, :, cols].rearrange("p t n -> p n t"))
+
+        load_half(0)
+        damping(0)
+        damping(1)
+        round_w3(0)
+        damping(2)
         signal(0)
         signal(1)
         signal(2)
         project(0, 0)
-        damping(4)
+        round_w3(1)
+        damping(3)
         signal(3)
         project(0, 1)
+        round_w3(2)
         project(0, 2)
+        load_half(1)
+        damping(4)
         damping(5)
         signal(4)
         project(1, 0)

@@ -20,11 +20,20 @@ ALU = mybir.AluOpType
 
 CHUNK = 128
 HALF = 512
-SC_BASE = (0, 4, 1)
-MOVES_BEFORE_TABLE = {3: 1, 9: 2}
-A_BANKS = (4, 5, 6, 7, 6, 0, 1, 2)
-Y_BANKS = ((4, 5, 7), (3, 4, 2), (5, 6, 0))
+CHUNKS = S // CHUNK
+SC_BASE = (0, 16, 112)
 GROUPS = ((0, 256), (256, 256), (512, 512))
+Y_BANKS = ((0, 1, 2), (3, 4, 5), (6, 7, 4))
+KIB = 1024
+LAP = 64
+TAB_AT = (20 * KIB, 36 * KIB, 0)
+TAB_SC_AT = 15 * KIB
+W2_SC_AT = 16 * KIB
+W1_AT = (20 * KIB, 28 * KIB, 36 * KIB)
+W3_AT = 44 * KIB
+BY_AT = 50 * KIB
+WGO_AT = 50 * KIB + LAP
+ABS_AT = (56 * KIB, 60 * KIB, W3_AT, W3_AT)
 
 
 def tile_list_predicate_damped_store_kernel(
@@ -33,97 +42,88 @@ def tile_list_predicate_damped_store_kernel(
     nc = tc.nc
     with ExitStack() as ctx:
         keep = ctx.enter_context(tc.tile_pool(name="keep", bufs=1))
+        shared = ctx.enter_context(tc.tile_pool(name="shared", bufs=1))
         ring = ctx.enter_context(tc.tile_pool(name="ring", bufs=2))
         psum = ctx.enter_context(tc.psum_pool(name="psum", bufs=1))
 
-        def held(shape, dtype, name):
-            return keep.tile(shape, dtype, name=name, align_bytes=64)
+        def held(shape, dtype, name, tag=None):
+            return keep.tile(shape, dtype, name=name, tag=tag or name, align_bytes=64)
+
+        def placed(shape, dtype, name, offset):
+            return shared.tile(shape, dtype, name=name, offset=offset, align_bytes=64)
 
         idx = keep.tile([P, S // 16], U16, name="idx")
         idx2 = keep.tile([P, S // 16], U16, name="idx2")
-        tab = [held([P, T], I32, "tab%d" % a) for a in range(PASSES)]
-        tab_sc = held([P, T // 4], I32, "tab_sc")
+        tab = [placed([P, T], I32, "tab%d" % a, TAB_AT[a]) for a in range(PASSES)]
+        tab_sc = placed([P, T // 4], I32, "tab_sc", TAB_SC_AT)
         w2_raw = held([P, PASSES, H // 2], I32, "w2_raw")
         w2_sc_raw = held([P, PASSES, H // 4], I32, "w2_sc_raw")
-        w1_first = held([P, 4, H], F32, "w1_first")
-        w1_raw = {}
-        for a in range(1, PASSES):
-            for u in range(2):
-                w1_raw[a, u] = held([P, 4, H // 2], F32, "w1_raw%d_%d" % (a, u))
+        w1_raw = [placed([P, 4, H], F32, "w1_raw%d" % a, W1_AT[a]) for a in range(PASSES - 1)]
+        w1_last = [placed([P, 2, H], F32, "w1_last%d" % u, W1_AT[PASSES - 1] + 4 * KIB * u) for u in range(2)]
         v_packed = held([P, S // 4], I32, "v_packed")
-        w3_raw = held([P, 4, N], F32, "w3_raw")
-        wgo_sb = held([P, S], F32, "wgo_sb")
+        w3_raw = placed([P, 4, N], F32, "w3_raw", W3_AT)
+        wgo_sb = placed([P, S], F32, "wgo_sb", WGO_AT)
         w2_codes = held([P, PASSES, H // 2], I32, "w2_codes")
-        w2_sc = held([P, PASSES, H // 4], I32, "w2_sc")
-        by_sb = held([P, N // P], F32, "by_sb")
+        w2_sc = placed([P, PASSES, H // 4], I32, "w2_sc", W2_SC_AT)
+        by_sb = placed([P, N // P], F32, "by_sb", BY_AT)
         v_sc = [held([P, S // 4], I32, "v_sc%d" % a) for a in range(PASSES)]
         warm_in = held([P, 1], F32, "warm_in")
         warm_out = held([P, 1], F32, "warm_out")
 
-        nc.gpsimd.memset(tab_sc[:], 0)
-        for a in range(PASSES):
-            nc.gpsimd.memset(v_sc[a][:], 0)
-        nc.gpsimd.memset(w2_sc[:], 0)
         nc.vector.memset(warm_in[:], 1.0)
         nc.scalar.activation(warm_out[:], warm_in[:], ACT.Abs_reciprocal_sqrt)
+        nc.gpsimd.memset(tab_sc[32:64, :], 0)
+        nc.gpsimd.memset(tab_sc[64:112, :], 0)
+        cache = [held([P, T2], F32, "cache%d" % n) for n in range(N // P)]
+        for zeroed in cache:
+            nc.gpsimd.memset(zeroed[:], 0.0)
+        for a in range(PASSES):
+            nc.vector.memset(v_sc[a][:], 0)
 
         def load_w1(a):
             rows = w1[512 * a : 512 * (a + 1), :].rearrange("(p j) c -> p j c", j=4)
-            if a == 0:
-                nc.sync.dma_start(w1_first[:], rows)
+            if a < PASSES - 1:
+                nc.sync.dma_start(w1_raw[a][:], rows)
             else:
                 for u in range(2):
-                    nc.sync.dma_start(w1_raw[a, u][:], rows[:, :, u * H // 2 : (u + 1) * H // 2])
+                    nc.sync.dma_start(w1_last[u][:], rows[:, 2 * u : 2 * u + 2, :])
 
         def load_table(a):
             nc.sync.dma_start(tab[a][:], tab_words[a].rearrange("p t i -> p (t i)").bitcast(I32))
 
-        def load_w2_scales(quad):
+        nc.sync.dma_start(idx[:], offs)
+        nc.sync.dma_start(tab_sc[0:32, :], tab_scales[0:2].rearrange("a q t -> (a q) t").bitcast(I32))
+        nc.sync.dma_start(tab_sc[112:128, :], tab_scales[2].bitcast(I32))
+        nc.sync.dma_start(w2_raw[:], w2_words.rearrange("a p b -> p a b").bitcast(I32))
+        load_table(0)
+        for quad in range(4):
             nc.sync.dma_start(
                 w2_sc_raw[32 * quad : 32 * quad + 4, :, :],
                 w2_scales[:, 4 * quad : 4 * quad + 4, :].rearrange("a r c -> r a c").bitcast(I32),
             )
-
-        nc.sync.dma_start(idx[:], offs)
-        nc.sync.dma_start(w2_raw[:], w2_words.rearrange("a p b -> p a b").bitcast(I32))
-        for a in range(PASSES):
-            nc.sync.dma_start(tab_sc[SC_BASE[a] : P : 8, :], tab_scales[a].bitcast(I32))
-        load_w2_scales(0)
-        load_w1(0)
-        load_table(0)
-        for quad in range(1, 4):
-            load_w2_scales(quad)
+        nc.sync.dma_start(idx2[:], offs2)
+        load_table(1)
 
         nc.vector.tensor_copy(v_packed[:].bitcast(U8), tab_sc[:].bitcast(U8).indirect(idx[:]))
         moves = [(a, r) for a in range(PASSES) for r in range(4)]
         for k, (a, r) in enumerate(moves):
-            if k in MOVES_BEFORE_TABLE:
-                load_table(MOVES_BEFORE_TABLE[k])
-            nc.sync.dma_start(v_sc[a][r:P:32, :], v_packed[SC_BASE[a] + 8 * r : P : 32, :])
+            if k == len(moves) // 2:
+                load_table(2)
+            nc.sync.dma_start(v_sc[a][r:P:32, :], v_packed[SC_BASE[a] + r : SC_BASE[a] + 16 : 4, :])
 
         v_halves = {}
 
-        def gather_words(a, first, width, tag):
-            gathered = keep.tile([P, width], I32, name="v_codes", tag=tag, align_bytes=64)
+        def gather_words(a, first, width):
+            gathered = held([P, width], I32, "v_codes%d_%d" % (a, first))
             cols = slice(first // 16, (first + width) // 16)
             nc.vector.tensor_copy(gathered[:].bitcast(U32), tab[a][:].bitcast(U32).indirect(idx[:, cols]))
             for c in range(0, width, HALF):
                 v_halves[a, (first + c) // HALF] = gathered[:, c : c + HALF]
 
-        gather_words(0, 0, S, "v_codes0")
-        gather_words(1, 0, S, "v_codes1")
-        gather_words(2, 0, HALF, "v_codes2")
-
-        for a in range(1, PASSES):
-            load_w1(a)
-        w3_rows = w3.rearrange("(q t i) n -> t q i n", t=4, i=8)
-        for t in range(4):
-            nc.sync.dma_start(w3_raw[:, t, :], w3_rows[t])
-        nc.sync.dma_start(wgo_sb[:], wgo)
-        nc.sync.dma_start(idx2[:], offs2)
-        with nc.allow_non_contiguous_dma(reason="one bias value a partition"):
-            nc.sync.dma_start(by_sb[:], by.rearrange("(n p) -> p n", p=P))
-
+        nc.vector.memset(w2_sc[:], 0)
+        gather_words(0, 0, S)
+        load_w1(0)
+        load_w1(1)
         nc.vector.tensor_copy(
             w2_codes[:].rearrange("p a (t q w) -> p a t q w", t=4, w=4),
             w2_raw[:].rearrange("p a (q t w) -> p a t q w", t=4, w=4),
@@ -134,126 +134,127 @@ def tile_list_predicate_damped_store_kernel(
                 w2_sc[rows].rearrange("p a (t q w) -> p a t q w", t=4, w=2),
                 w2_sc_raw[rows].rearrange("p a (q t w) -> p a t q w", t=4, w=2),
             )
-
-        def rhs(a, g):
-            half, start = divmod(g * CHUNK, HALF)
-            codes = v_halves[a, half][:, start : start + CHUNK].bitcast(FP8X4)
-            scales = v_sc[a][:].bitcast(U8)[:, g * CHUNK : (g + 1) * CHUNK]
-            return codes, scales
+        gather_words(1, 0, S)
+        load_w1(2)
+        w3_rows = w3.rearrange("(q t i) n -> t q i n", t=4, i=8)
+        for t in range(4):
+            nc.sync.dma_start(w3_raw[:, t, :], w3_rows[t])
+        nc.sync.dma_start(wgo_sb[:], wgo)
+        with nc.allow_non_contiguous_dma(reason="one bias value a partition"):
+            nc.sync.dma_start(by_sb[:], by.rearrange("(n p) -> p n", p=P))
+        gather_words(2, 0, HALF)
+        gather_words(2, HALF, HALF)
 
         w1_codes = held([P, PASSES, H], U32, "w1_codes")
         w1_sc = held([P, PASSES, H], U8, "w1_sc")
-        w1_bf = [held([P, H, 4], BF16, "w1_bf%d" % a) for a in range(PASSES)]
-        for a in range(PASSES):
-            dst = w1_bf[a][:].rearrange("p (t q i) j -> p t q i j", t=4, i=8)
-            flat = w1_bf[a][:].rearrange("p m j -> p (m j)")
-            if a == 0:
-                nc.vector.tensor_copy(dst, w1_first[:].rearrange("p j (q t i) -> p t q i j", t=4, i=8))
-            else:
-                for u in range(2):
-                    nc.vector.tensor_copy(
-                        dst[:, :, 8 * u : 8 * (u + 1)], w1_raw[a, u][:].rearrange("p j (q t i) -> p t q i j", t=4, i=8)
-                    )
+
+        def prepare_w1(a, pieces):
+            rounded = [held([P, H // 2, 4], BF16, "w1_bf%d_%d" % (a, u)) for u in range(2)]
+            dst = [rounded[u][:].rearrange("p (t q i) j -> p t q i j", t=2, i=8) for u in range(2)]
             if a < PASSES - 1:
-                nc.vector.quantize_mx(w1_codes[:, a, :].bitcast(FP8X4), w1_sc[:, a, :], flat)
+                src = w1_raw[a][:].rearrange("p j (q t i) -> p t q i j", t=4, i=8)
+                for u in range(2):
+                    nc.vector.tensor_copy(dst[u], src[:, 2 * u : 2 * u + 2])
             else:
-                for t in range(4):
-                    cols = slice(P * t, P * (t + 1))
-                    nc.vector.quantize_mx(
-                        w1_codes[:, a, cols].bitcast(FP8X4), w1_sc[:, a, cols], flat[:, 512 * t : 512 * (t + 1)]
-                    )
-        gather_words(2, HALF, HALF, "w1_raw2_1")
+                for pair in range(2):
+                    src = w1_last[pair][:].rearrange("p j (q t i) -> p t q i j", t=4, i=8)
+                    for u in range(2):
+                        nc.vector.tensor_copy(dst[u][:, :, :, :, 2 * pair : 2 * pair + 2], src[:, 2 * u : 2 * u + 2])
+            width = H // pieces
+            for first in range(0, H, width):
+                u, start = divmod(first, H // 2)
+                cols = slice(first, first + width)
+                nc.vector.quantize_mx(
+                    w1_codes[:, a, cols].bitcast(FP8X4),
+                    w1_sc[:, a, cols],
+                    rounded[u][:, start : start + width, :].rearrange("p m j -> p (m j)"),
+                )
 
-        cache = []
-        for tag in ("tab_sc", "w1_first", "tab0"):
-            zeroed = keep.tile([P, T2], F32, name="cache", tag=tag, align_bytes=64)
-            nc.gpsimd.memset(zeroed[:], 0.0)
-            cache.append(zeroed)
-
-        w3_codes = held([P, N], U32, "w3_codes")
-        w3_sc = held([P, N], U8, "w3_sc")
-        w3_bf = held([P, N, 4], BF16, "w3_bf")
-
-        b_abs = [held([P, 4, HALF], F32, "b_abs%d" % half) for half in range(S // HALF)]
-
-        def load_half(half):
-            for t in range(4):
-                b_ps = psum.tile([P, HALF], F32, name="b_ps", tag="bank%d" % t)
-                for a in range(PASSES):
-                    nc.tensor.matmul_mx(
-                        b_ps[:],
-                        lhsT=w2_codes[:, a, 64 * t : 64 * (t + 1)].bitcast(U8).bitcast(FP4X4),
-                        lhsT_scale=w2_sc[:, a, 32 * t : 32 * (t + 1)].bitcast(U8),
-                        rhs=v_halves[a, half].bitcast(FP8X4),
-                        rhs_scale=v_sc[a][:].bitcast(U8)[:, half * HALF : (half + 1) * HALF],
-                        start=(a == 0),
-                        stop=(a == PASSES - 1),
-                    )
-                nc.scalar.activation(b_abs[half][:, t, :], b_ps[:], ACT.Abs)
-
-        damp = []
-        for g in range(S // CHUNK):
-            damp.append(held([P, CHUNK, 4], F32, "damp%d" % g))
-
-        def damping(g):
+        def product_pass(acc, g, a, stationary):
             half, start = divmod(g * CHUNK, HALF)
-            root = ring.tile([P, CHUNK, 4], F32, name="root")
-            nc.scalar.activation(
-                root[:],
-                b_abs[half][:, :, start : start + CHUNK].rearrange("p t n -> p n t"),
-                ACT.Abs_reciprocal_sqrt,
-                bias=warm_out[:],
+            for t in range(4):
+                codes, scales = stationary(a, t)
+                nc.tensor.matmul_mx(
+                    acc[:, t, :],
+                    lhsT=codes,
+                    lhsT_scale=scales,
+                    rhs=v_halves[a, half][:, start : start + CHUNK].bitcast(FP8X4),
+                    rhs_scale=v_sc[a][:].bitcast(U8)[:, g * CHUNK : (g + 1) * CHUNK],
+                    start=(a == 0 and t == 0),
+                    stop=(a == PASSES - 1 and t == 3),
+                )
+
+        def w2_tile(a, t):
+            return (
+                w2_codes[:, a, 64 * t : 64 * (t + 1)].bitcast(U8).bitcast(FP4X4),
+                w2_sc[:, a, 32 * t : 32 * (t + 1)].bitcast(U8),
             )
-            nc.scalar.activation(damp[g][:], root[:], ACT.Square)
+
+        def w1_tile(a, t):
+            cols = slice(P * t, P * (t + 1))
+            return w1_codes[:, a, cols].bitcast(FP8X4), w1_sc[:, a, cols]
+
+        def products(chunks, first_bank, stationary, name):
+            accs = {}
+            for g in chunks:
+                accs[g] = psum.tile([P, 4, CHUNK], F32, name=name, tag="bank%d" % (first_bank + g % 4))
+            for a in range(PASSES):
+                for g in chunks:
+                    product_pass(accs[g], g, a, stationary)
+            return accs
+
+        damp = [held([P, CHUNK, 4], F32, "damp%d" % g) for g in range(CHUNKS)]
+
+        def damping(b_ps, g):
+            size = placed([P, 2, CHUNK, 4], F32, "b_abs%d" % g, ABS_AT[g // 2])
+            for u in range(2):
+                nc.scalar.activation(size[:, u], b_ps[g + u][:].rearrange("p t n -> p n t"), ACT.Abs)
+            for u in range(2):
+                root = ring.tile([P, CHUNK, 4], F32, name="root")
+                nc.scalar.activation(root[:], size[:, u], ACT.Abs_reciprocal_sqrt, bias=warm_out[:])
+                nc.scalar.activation(damp[g + u][:], root[:], ACT.Square)
 
         h_bf = [held([P, count, 4], BF16, "h_bf%d" % first) for first, count in GROUPS]
         h_codes = [held([P, count], U32, "h_codes%d" % first) for first, count in GROUPS]
         h_sc = [held([P, count], U8, "h_sc%d" % first) for first, count in GROUPS]
+        w3_codes = {}
+        w3_sc = [held([P, P], U8, "w3_sc%d" % n) for n in range(N // P)]
+        w3_bf = [placed([P, P, 4], BF16, "w3_bf%d" % n, ABS_AT[1] + n * KIB) for n in range(N // P)]
 
-        def signal(g):
+        def damped(a_ps, g):
             group = max(k for k in range(len(GROUPS)) if GROUPS[k][0] <= g * CHUNK)
             first, count = GROUPS[group]
-            a_ps = psum.tile([P, 4, CHUNK], F32, name="a_ps", tag="bank%d" % A_BANKS[g])
-            for t in range(4):
-                cols = slice(P * t, P * (t + 1))
-                for a in range(PASSES):
-                    codes, scales = rhs(a, g)
-                    nc.tensor.matmul_mx(
-                        a_ps[:, t, :],
-                        lhsT=w1_codes[:, a, cols].bitcast(FP8X4),
-                        lhsT_scale=w1_sc[:, a, cols],
-                        rhs=codes,
-                        rhs_scale=scales,
-                        start=(a == 0),
-                        stop=(a == PASSES - 1),
-                    )
             start = g * CHUNK - first
             nc.vector.tensor_tensor(
-                h_bf[group][:, start : start + CHUNK, :], a_ps[:].rearrange("p t n -> p n t"), damp[g][:], ALU.mult
+                h_bf[group][:, start : start + CHUNK, :], a_ps[g][:].rearrange("p t n -> p n t"), damp[g][:], ALU.mult
             )
             if start + CHUNK == count:
                 nc.vector.quantize_mx(
                     h_codes[group][:].bitcast(FP8X4), h_sc[group][:], h_bf[group][:].rearrange("p n t -> p (n t)")
                 )
 
-        def project(group, n):
+        def prepare_w3(n, after):
+            cols = slice(P * n, P * (n + 1))
+            w3_codes[n] = held([P, P], U32, "w3_codes%d" % n, "damp%d" % after)
+            nc.scalar.copy(w3_bf[n][:], w3_raw[:, :, cols].rearrange("p t n -> p n t"))
+            nc.vector.quantize_mx(
+                w3_codes[n][:].bitcast(FP8X4), w3_sc[n][:], w3_bf[n][:].rearrange("p n t -> p (n t)")
+            )
+
+        def project(group, n, tag=None):
             first, count = GROUPS[group]
             cols = slice(P * n, P * (n + 1))
-            if group == 0:
-                nc.vector.quantize_mx(
-                    w3_codes[:, cols].bitcast(FP8X4), w3_sc[:, cols], w3_bf[:, cols, :].rearrange("p n t -> p (n t)")
-                )
             y_ps = psum.tile([P, count], F32, name="y_ps", tag="bank%d" % Y_BANKS[group][n])
             nc.tensor.matmul_mx(
                 y_ps[:],
-                lhsT=w3_codes[:, cols].bitcast(FP8X4),
-                lhsT_scale=w3_sc[:, cols],
+                lhsT=w3_codes[n][:].bitcast(FP8X4),
+                lhsT_scale=w3_sc[n][:],
                 rhs=h_codes[group][:].bitcast(FP8X4),
                 rhs_scale=h_sc[group][:],
                 start=True,
                 stop=True,
             )
-            y_sb = held([P, count], F32, "y_sb%d_%d" % (group, n))
+            y_sb = held([P, count], F32, "y_sb%d_%d" % (group, n), tag)
             nc.scalar.activation(y_sb[:], y_ps[:], ACT.Identity, bias=by_sb[:, n : n + 1])
             nc.vector.tensor_tensor(
                 cache[n][:].indirect(idx2[:, first // 16 : (first + count) // 16]),
@@ -264,36 +265,35 @@ def tile_list_predicate_damped_store_kernel(
             if first + count == S:
                 nc.sync.dma_start(out[cols, :], cache[n][:])
 
-        def round_w3(n):
-            cols = slice(P * n, P * (n + 1))
-            nc.scalar.copy(w3_bf[:, cols, :], w3_raw[:, :, cols].rearrange("p t n -> p n t"))
-
-        load_half(0)
-        damping(0)
-        damping(1)
-        round_w3(0)
-        damping(2)
-        signal(0)
-        signal(1)
-        signal(2)
+        b_first = products(range(0, 4), 0, w2_tile, "b_ps")
+        damping(b_first, 0)
+        damping(b_first, 2)
+        prepare_w1(0, 2)
+        prepare_w1(1, 2)
+        prepare_w1(2, 4)
+        a_first = products(range(0, 4), 4, w1_tile, "a_ps")
+        damped(a_first, 0)
+        damped(a_first, 1)
+        prepare_w3(0, 0)
         project(0, 0)
-        round_w3(1)
-        damping(3)
-        signal(3)
+        damped(a_first, 2)
+        damped(a_first, 3)
+        prepare_w3(1, 2)
         project(0, 1)
-        round_w3(2)
+        prepare_w3(2, 3)
         project(0, 2)
-        load_half(1)
-        damping(4)
-        damping(5)
-        signal(4)
         project(1, 0)
-        damping(6)
-        signal(5)
-        damping(7)
-        signal(6)
+        b_second = {}
+        for g in range(4, 8):
+            b_second.update(products([g], 0, w2_tile, "b_ps"))
+        damping(b_second, 4)
         project(1, 1)
-        signal(7)
-        project(1, 2)
+        damping(b_second, 6)
+        a_second = {}
+        for g in range(4, 8):
+            a_second.update(products([g], 0, w1_tile, "a_ps"))
+        for g in range(4, 8):
+            damped(a_second, g)
+        project(1, 2, "damp7")
         for n in range(N // P):
             project(2, n)

@@ -152,9 +152,11 @@ def tile_list_predicate_damped_store_kernel(
             rounded = [held([P, H // 2, 4], BF16, "w1_bf%d_%d" % (a, u)) for u in range(2)]
             dst = [rounded[u][:].rearrange("p (t q i) j -> p t q i j", t=2, i=8) for u in range(2)]
             if a < PASSES - 1:
-                src = w1_raw[a][:].rearrange("p j (q t i) -> p t q i j", t=4, i=8)
+                src = w1_raw[a][:].rearrange("p j (q t i) -> p t q j i", t=4, i=8)
                 for u in range(2):
-                    nc.vector.tensor_copy(dst[u], src[:, 2 * u : 2 * u + 2])
+                    nc.vector.tensor_copy(
+                        rounded[u][:].rearrange("p (t q i) j -> p t q j i", t=2, i=8), src[:, 2 * u : 2 * u + 2]
+                    )
             else:
                 for pair in range(2):
                     src = w1_last[pair][:].rearrange("p j (q t i) -> p t q i j", t=4, i=8)

@@ -139,9 +139,9 @@ def tile_list_predicate_damped_store_kernel(
         w3_rows = w3.rearrange("(q t i) n -> t q i n", t=4, i=8)
         for t in range(4):
             nc.sync.dma_start(w3_raw[:, t, :], w3_rows[t])
-        nc.sync.dma_start(wgo_sb[:], wgo)
         with nc.allow_non_contiguous_dma(reason="one bias value a partition"):
             nc.sync.dma_start(by_sb[:], by.rearrange("(n p) -> p n", p=P))
+        nc.sync.dma_start(wgo_sb[:], wgo)
         gather_words(2, 0, HALF)
         gather_words(2, HALF, HALF)
 

@@ -22,8 +22,9 @@ CHUNK = 128
 HALF = 512
 CHUNKS = S // CHUNK
 SC_BASE = (0, 16, 112)
-GROUPS = ((0, 256), (256, 256), (512, 512))
-Y_BANKS = ((0, 1, 2), (3, 4, 5), (6, 7, 4))
+GROUP = 256
+LATE_BANKS = {4: 0, 5: 1, 6: 6, 7: 7}
+ON_GPSIMD = (4, 5, 6)
 KIB = 1024
 LAP = 64
 TAB_AT = (20 * KIB, 36 * KIB, 0)
@@ -33,7 +34,7 @@ W1_AT = (20 * KIB, 28 * KIB, 36 * KIB)
 W3_AT = 44 * KIB
 BY_AT = 50 * KIB
 WGO_AT = 50 * KIB + LAP
-ABS_AT = (56 * KIB, 60 * KIB, W3_AT, W3_AT)
+ABS_AT = (56 * KIB, 60 * KIB, W3_AT, 64 * KIB)
 
 
 def tile_list_predicate_damped_store_kernel(
@@ -77,6 +78,10 @@ def tile_list_predicate_damped_store_kernel(
         cache = [held([P, T2], F32, "cache%d" % n) for n in range(N // P)]
         for zeroed in cache:
             nc.gpsimd.memset(zeroed[:], 0.0)
+        warm_f32 = held([P, CHUNK], F32, "warm_f32")
+        warm_bf = held([P, CHUNK], BF16, "warm_bf")
+        nc.gpsimd.tensor_tensor(warm_f32[:], cache[2][:, 0:CHUNK], cache[2][:, CHUNK : 2 * CHUNK], ALU.mult)
+        nc.gpsimd.tensor_tensor(warm_bf[:], cache[2][:, 0:CHUNK], cache[2][:, CHUNK : 2 * CHUNK], ALU.mult)
         for a in range(PASSES):
             nc.vector.memset(v_sc[a][:], 0)
 
@@ -199,7 +204,8 @@ def tile_list_predicate_damped_store_kernel(
         def products(chunks, first_bank, stationary, name):
             accs = {}
             for g in chunks:
-                accs[g] = psum.tile([P, 4, CHUNK], F32, name=name, tag="bank%d" % (first_bank + g % 4))
+                bank = LATE_BANKS.get(g, first_bank + g)
+                accs[g] = psum.tile([P, 4, CHUNK], F32, name=name, tag="bank%d" % bank)
             for a in range(PASSES):
                 for g in chunks:
                     product_pass(accs[g], g, a, stationary)
@@ -207,33 +213,57 @@ def tile_list_predicate_damped_store_kernel(
 
         damp = [held([P, CHUNK, 4], F32, "damp%d" % g) for g in range(CHUNKS)]
 
-        def damping(b_ps, g):
+        sizes = {}
+
+        def magnitudes(b_ps, g):
             size = placed([P, 2, CHUNK, 4], F32, "b_abs%d" % g, ABS_AT[g // 2])
             for u in range(2):
                 nc.scalar.activation(size[:, u], b_ps[g + u][:].rearrange("p t n -> p n t"), ACT.Abs)
-            for u in range(2):
-                root = ring.tile([P, CHUNK, 4], F32, name="root")
-                nc.scalar.activation(root[:], size[:, u], ACT.Abs_reciprocal_sqrt, bias=warm_out[:])
-                nc.scalar.activation(damp[g + u][:], root[:], ACT.Square)
+                sizes[g + u] = size[:, u]
 
-        h_bf = [held([P, count, 4], BF16, "h_bf%d" % first) for first, count in GROUPS]
-        h_codes = [held([P, count], U32, "h_codes%d" % first) for first, count in GROUPS]
-        h_sc = [held([P, count], U8, "h_sc%d" % first) for first, count in GROUPS]
+        roots = {}
+
+        def root_of(g):
+            if g == CHUNKS - 1:
+                roots[g] = held([P, CHUNK, 4], F32, "root7")
+            else:
+                roots[g] = ring.tile([P, CHUNK, 4], F32, name="root")
+            nc.scalar.activation(roots[g][:], sizes[g], ACT.Abs_reciprocal_sqrt, bias=warm_out[:])
+
+        def square_of(g):
+            nc.scalar.activation(damp[g][:], roots[g][:], ACT.Square)
+
+        def damping(b_ps, g):
+            magnitudes(b_ps, g)
+            root_of(g)
+            root_of(g + 1)
+            square_of(g)
+            square_of(g + 1)
+
+        h_bf = {}
+        h_codes = held([P, S], U32, "h_codes")
+        h_sc = held([P, S], U8, "h_sc")
         w3_codes = {}
         w3_sc = [held([P, P], U8, "w3_sc%d" % n) for n in range(N // P)]
         w3_bf = [placed([P, P, 4], BF16, "w3_bf%d" % n, ABS_AT[1] + n * KIB) for n in range(N // P)]
 
+        a_sb = {g: held([P, CHUNK, 4], F32, "a_sb%d" % g) for g in ON_GPSIMD}
+
         def damped(a_ps, g):
-            group = max(k for k in range(len(GROUPS)) if GROUPS[k][0] <= g * CHUNK)
-            first, count = GROUPS[group]
-            start = g * CHUNK - first
-            nc.vector.tensor_tensor(
-                h_bf[group][:, start : start + CHUNK, :], a_ps[g][:].rearrange("p t n -> p n t"), damp[g][:], ALU.mult
+            group, u = divmod(g, 2)
+            if u == 0:
+                h_bf[group] = held([P, GROUP, 4], BF16, "h_bf%d" % group, "h_bf%d" % min(group, 2))
+            target = h_bf[group][:, u * CHUNK : (u + 1) * CHUNK, :]
+            if g in ON_GPSIMD:
+                nc.gpsimd.tensor_tensor(target, a_sb[g][:], damp[g][:], ALU.mult)
+            else:
+                nc.vector.tensor_tensor(target, a_ps[g][:].rearrange("p t n -> p n t"), damp[g][:], ALU.mult)
+
+        def quantise_h(group):
+            cols = slice(GROUP * group, GROUP * (group + 1))
+            nc.vector.quantize_mx(
+                h_codes[:, cols].bitcast(FP8X4), h_sc[:, cols], h_bf[group][:].rearrange("p n t -> p (n t)")
             )
-            if start + CHUNK == count:
-                nc.vector.quantize_mx(
-                    h_codes[group][:].bitcast(FP8X4), h_sc[group][:], h_bf[group][:].rearrange("p n t -> p (n t)")
-                )
 
         def prepare_w3(n, after):
             cols = slice(P * n, P * (n + 1))
@@ -243,59 +273,92 @@ def tile_list_predicate_damped_store_kernel(
                 w3_codes[n][:].bitcast(FP8X4), w3_sc[n][:], w3_bf[n][:].rearrange("p n t -> p (n t)")
             )
 
-        def project(group, n, tag=None):
-            first, count = GROUPS[group]
-            cols = slice(P * n, P * (n + 1))
-            y_ps = psum.tile([P, count], F32, name="y_ps", tag="bank%d" % Y_BANKS[group][n])
+        def projection(group, n, bank, groups=1):
+            cols = slice(GROUP * group, GROUP * (group + groups))
+            y_ps = psum.tile([P, GROUP * groups], F32, name="y_ps", tag="bank%d" % bank)
             nc.tensor.matmul_mx(
                 y_ps[:],
                 lhsT=w3_codes[n][:].bitcast(FP8X4),
                 lhsT_scale=w3_sc[n][:],
-                rhs=h_codes[group][:].bitcast(FP8X4),
-                rhs_scale=h_sc[group][:],
+                rhs=h_codes[:, cols].bitcast(FP8X4),
+                rhs_scale=h_sc[:, cols],
                 start=True,
                 stop=True,
             )
-            y_sb = held([P, count], F32, "y_sb%d_%d" % (group, n), tag)
-            nc.scalar.activation(y_sb[:], y_ps[:], ACT.Identity, bias=by_sb[:, n : n + 1])
-            nc.vector.tensor_tensor(
-                cache[n][:].indirect(idx2[:, first // 16 : (first + count) // 16]),
-                y_sb[:],
-                wgo_sb[:, first : first + count],
-                ALU.mult,
-            )
-            if first + count == S:
-                nc.sync.dma_start(out[cols, :], cache[n][:])
+            return y_ps
 
-        b_first = products(range(0, 4), 0, w2_tile, "b_ps")
-        damping(b_first, 0)
-        damping(b_first, 2)
+        def places(group, n, groups=1):
+            return cache[n][:].indirect(idx2[:, GROUP * group // 16 : GROUP * (group + groups) // 16])
+
+        def weights(group, groups=1):
+            return wgo_sb[:, GROUP * group : GROUP * (group + groups)]
+
+        def biased(group, n, bank, tag=None, groups=1):
+            y_ps = projection(group, n, bank, groups)
+            y_sb = held([P, GROUP * groups], F32, "y_sb%d_%d" % (group, n), tag)
+            nc.scalar.activation(y_sb[:], y_ps[:], ACT.Identity, bias=by_sb[:, n : n + 1])
+            return y_sb
+
+        def scatter_product(group, n, y_sb, groups=1):
+            nc.vector.tensor_tensor(places(group, n, groups), y_sb[:], weights(group, groups), ALU.mult)
+            if group + groups == S // GROUP:
+                nc.sync.dma_start(out[P * n : P * (n + 1), :], cache[n][:])
+
+        def late_pair(pair):
+            for g in (pair, pair + 1):
+                b_ps.update(products([g], 0, w2_tile, "b_ps"))
+            magnitudes(b_ps, pair)
+            for g in (pair, pair + 1):
+                a_ps.update(products([g], 0, w1_tile, "a_ps"))
+                root_of(g)
+                if g in ON_GPSIMD:
+                    nc.scalar.copy(a_sb[g][:], a_ps[g][:].rearrange("p t n -> p n t"))
+                square_of(g)
+
+        b_ps = products(range(0, 4), 0, w2_tile, "b_ps")
+        damping(b_ps, 0)
+        damping(b_ps, 2)
         prepare_w1(0, 2)
         prepare_w1(1, 2)
         prepare_w1(2, 4)
-        a_first = products(range(0, 4), 4, w1_tile, "a_ps")
-        damped(a_first, 0)
-        damped(a_first, 1)
+        a_ps = products(range(0, 4), 4, w1_tile, "a_ps")
+        damped(a_ps, 0)
+        damped(a_ps, 1)
         prepare_w3(0, 0)
-        project(0, 0)
-        damped(a_first, 2)
-        damped(a_first, 3)
-        prepare_w3(1, 2)
-        project(0, 1)
-        prepare_w3(2, 3)
-        project(0, 2)
-        project(1, 0)
-        b_second = {}
-        for g in range(4, 8):
-            b_second.update(products([g], 0, w2_tile, "b_ps"))
-        damping(b_second, 4)
-        project(1, 1)
-        damping(b_second, 6)
-        a_second = {}
-        for g in range(4, 8):
-            a_second.update(products([g], 0, w1_tile, "a_ps"))
-        for g in range(4, 8):
-            damped(a_second, g)
-        project(1, 2, "damp7")
-        for n in range(N // P):
-            project(2, n)
+        quantise_h(0)
+        y_first = biased(0, 0, 2, "y_first")
+        prepare_w3(1, 1)
+        damped(a_ps, 2)
+        damped(a_ps, 3)
+        prepare_w3(2, 2)
+        quantise_h(1)
+        y_second = projection(0, 1, 3)
+        weighted_second = held([P, GROUP], F32, "weighted_second")
+        nc.vector.scalar_tensor_tensor(
+            weighted_second[:], y_second[:], by_sb[:, 1:2], weights(0), ALU.add, ALU.mult
+        )
+        scatter_product(0, 0, y_first)
+        nc.vector.tensor_copy(places(0, 1), weighted_second[:])
+        copied = ((0, 2, 4), (1, 0, 5), (1, 1, 2))
+        y_copied = [biased(group, n, bank) for group, n, bank in copied]
+        weighted = held([P, 3, GROUP], F32, "weighted", "y_first")
+        for k, (group, n, bank) in enumerate(copied):
+            nc.gpsimd.tensor_tensor(weighted[:, k, :], y_copied[k][:], weights(group), ALU.mult)
+            nc.vector.tensor_copy(places(group, n), weighted[:, k, :])
+        late_pair(4)
+        damped(a_ps, 4)
+        damped(a_ps, 5)
+        quantise_h(2)
+        y_held = biased(1, 2, 3)
+        weighted_held = held([P, GROUP], F32, "weighted_held", "damp5")
+        nc.gpsimd.tensor_tensor(weighted_held[:], y_held[:], weights(1), ALU.mult)
+        nc.vector.tensor_copy(places(1, 2), weighted_held[:])
+        late_pair(6)
+        damped(a_ps, 6)
+        damped(a_ps, 7)
+        scatter_product(2, 0, biased(2, 0, 4, "root7"))
+        quantise_h(3)
+        scatter_product(2, 1, biased(2, 1, 5, "damp7"))
+        scatter_product(3, 0, biased(3, 0, 2))
+        scatter_product(3, 1, biased(3, 1, 3))
+        scatter_product(2, 2, biased(2, 2, 4, groups=2), groups=2)

@@ -23,7 +23,8 @@ HALF = 512
 CHUNKS = S // CHUNK
 SC_BASE = (0, 16, 112)
 GROUP = 256
-LATE_BANKS = {4: 0, 5: 1, 6: 6, 7: 7}
+B_BANKS = (0, 1, 2, 3, 0, 1, 6, 7)
+A_BANKS = (4, 5, 6, 7, 4, 5, 6, 7)
 ON_GPSIMD = (4, 5, 6)
 KIB = 1024
 LAP = 64
@@ -34,7 +35,8 @@ W1_AT = (20 * KIB, 28 * KIB, 36 * KIB)
 W3_AT = 44 * KIB
 BY_AT = 50 * KIB
 WGO_AT = 50 * KIB + LAP
-ABS_AT = (56 * KIB, 60 * KIB, W3_AT, 64 * KIB)
+ABS_AT = (56 * KIB, 60 * KIB, 56 * KIB, 64 * KIB)
+ROOT_LAST_AT = 72 * KIB
 
 
 def tile_list_predicate_damped_store_kernel(
@@ -78,10 +80,6 @@ def tile_list_predicate_damped_store_kernel(
         cache = [held([P, T2], F32, "cache%d" % n) for n in range(N // P)]
         for zeroed in cache:
             nc.gpsimd.memset(zeroed[:], 0.0)
-        warm_f32 = held([P, CHUNK], F32, "warm_f32")
-        warm_bf = held([P, CHUNK], BF16, "warm_bf")
-        nc.gpsimd.tensor_tensor(warm_f32[:], cache[2][:, 0:CHUNK], cache[2][:, CHUNK : 2 * CHUNK], ALU.mult)
-        nc.gpsimd.tensor_tensor(warm_bf[:], cache[2][:, 0:CHUNK], cache[2][:, CHUNK : 2 * CHUNK], ALU.mult)
         for a in range(PASSES):
             nc.vector.memset(v_sc[a][:], 0)
 
@@ -201,17 +199,16 @@ def tile_list_predicate_damped_store_kernel(
             cols = slice(P * t, P * (t + 1))
             return w1_codes[:, a, cols].bitcast(FP8X4), w1_sc[:, a, cols]
 
-        def products(chunks, first_bank, stationary, name):
+        def products(chunks, banks, stationary, name):
             accs = {}
             for g in chunks:
-                bank = LATE_BANKS.get(g, first_bank + g)
-                accs[g] = psum.tile([P, 4, CHUNK], F32, name=name, tag="bank%d" % bank)
+                accs[g] = psum.tile([P, 4, CHUNK], F32, name=name, tag="bank%d" % banks[g])
             for a in range(PASSES):
                 for g in chunks:
                     product_pass(accs[g], g, a, stationary)
             return accs
 
-        damp = [held([P, CHUNK, 4], F32, "damp%d" % g) for g in range(CHUNKS)]
+        damp = {g: held([P, CHUNK, 4], F32, "damp%d" % g) for g in range(CHUNKS) if g != 3}
 
         sizes = {}
 
@@ -225,7 +222,9 @@ def tile_list_predicate_damped_store_kernel(
 
         def root_of(g):
             if g == CHUNKS - 1:
-                roots[g] = held([P, CHUNK, 4], F32, "root7")
+                roots[g] = placed([P, CHUNK, 4], F32, "root7", ROOT_LAST_AT)
+            elif g >= 4:
+                roots[g] = placed([P, CHUNK, 4], F32, "root%d" % g, W3_AT + 2 * KIB * (g % 2))
             else:
                 roots[g] = ring.tile([P, CHUNK, 4], F32, name="root")
             nc.scalar.activation(roots[g][:], sizes[g], ACT.Abs_reciprocal_sqrt, bias=warm_out[:])
@@ -238,7 +237,8 @@ def tile_list_predicate_damped_store_kernel(
             root_of(g)
             root_of(g + 1)
             square_of(g)
-            square_of(g + 1)
+            if g == 0:
+                square_of(g + 1)
 
         h_bf = {}
         h_codes = held([P, S], U32, "h_codes")
@@ -249,15 +249,25 @@ def tile_list_predicate_damped_store_kernel(
 
         a_sb = {g: held([P, CHUNK, 4], F32, "a_sb%d" % g) for g in ON_GPSIMD}
 
-        def damped(a_ps, g):
+        h_full = {}
+
+        def h_target(g):
             group, u = divmod(g, 2)
-            if u == 0:
-                h_bf[group] = held([P, GROUP, 4], BF16, "h_bf%d" % group, "h_bf%d" % min(group, 2))
-            target = h_bf[group][:, u * CHUNK : (u + 1) * CHUNK, :]
-            if g in ON_GPSIMD:
-                nc.gpsimd.tensor_tensor(target, a_sb[g][:], damp[g][:], ALU.mult)
-            else:
-                nc.vector.tensor_tensor(target, a_ps[g][:].rearrange("p t n -> p n t"), damp[g][:], ALU.mult)
+            if u == 0 and group < 3:
+                h_bf[group] = held([P, GROUP, 4], BF16, "h_bf%d" % group)
+            elif u == 0:
+                h_bf[group] = placed([P, GROUP, 4], BF16, "h_bf%d" % group, ROOT_LAST_AT + KIB)
+            return h_bf[group][:, u * CHUNK : (u + 1) * CHUNK, :]
+
+        def damped(a_ps, g):
+            nc.vector.tensor_tensor(h_target(g), a_ps[g][:].rearrange("p t n -> p n t"), damp[g][:], ALU.mult)
+
+        def damped_full(g, tag=None):
+            h_full[g] = held([P, CHUNK, 4], F32, "h_full%d" % g, tag)
+            nc.gpsimd.tensor_tensor(h_full[g][:], a_sb[g][:], damp[g][:], ALU.mult)
+
+        def rounded_h(g):
+            nc.scalar.copy(h_target(g), h_full[g][:])
 
         def quantise_h(group):
             cols = slice(GROUP * group, GROUP * (group + 1))
@@ -293,9 +303,12 @@ def tile_list_predicate_damped_store_kernel(
         def weights(group, groups=1):
             return wgo_sb[:, GROUP * group : GROUP * (group + groups)]
 
-        def biased(group, n, bank, tag=None, groups=1):
+        def biased(group, n, bank, tag=None, groups=1, offset=None):
             y_ps = projection(group, n, bank, groups)
-            y_sb = held([P, GROUP * groups], F32, "y_sb%d_%d" % (group, n), tag)
+            if offset is None:
+                y_sb = held([P, GROUP * groups], F32, "y_sb%d_%d" % (group, n), tag)
+            else:
+                y_sb = placed([P, GROUP * groups], F32, "y_sb%d_%d" % (group, n), offset)
             nc.scalar.activation(y_sb[:], y_ps[:], ACT.Identity, bias=by_sb[:, n : n + 1])
             return y_sb
 
@@ -304,61 +317,81 @@ def tile_list_predicate_damped_store_kernel(
             if group + groups == S // GROUP:
                 nc.sync.dma_start(out[P * n : P * (n + 1), :], cache[n][:])
 
-        def late_pair(pair):
+        def late_loads(pair):
             for g in (pair, pair + 1):
-                b_ps.update(products([g], 0, w2_tile, "b_ps"))
+                b_ps.update(products([g], B_BANKS, w2_tile, "b_ps"))
             magnitudes(b_ps, pair)
-            for g in (pair, pair + 1):
-                a_ps.update(products([g], 0, w1_tile, "a_ps"))
-                root_of(g)
-                if g in ON_GPSIMD:
-                    nc.scalar.copy(a_sb[g][:], a_ps[g][:].rearrange("p t n -> p n t"))
-                square_of(g)
 
-        b_ps = products(range(0, 4), 0, w2_tile, "b_ps")
+        def late_signal(g):
+            a_ps.update(products([g], A_BANKS, w1_tile, "a_ps"))
+            if g in ON_GPSIMD:
+                nc.scalar.copy(a_sb[g][:], a_ps[g][:].rearrange("p t n -> p n t"))
+
+        def scatter_copy(group, n, y_sb, target):
+            nc.gpsimd.tensor_tensor(target, y_sb[:], weights(group), ALU.mult)
+            nc.vector.tensor_copy(places(group, n), target)
+
+        b_ps = products(range(0, 4), B_BANKS, w2_tile, "b_ps")
         damping(b_ps, 0)
         damping(b_ps, 2)
         prepare_w1(0, 2)
         prepare_w1(1, 2)
         prepare_w1(2, 4)
-        a_ps = products(range(0, 4), 4, w1_tile, "a_ps")
+        damp[3] = held([P, CHUNK, 4], F32, "damp3", "w1_bf2_1")
+        nc.gpsimd.tensor_tensor(damp[3][:], roots[3][:], roots[3][:], ALU.mult)
+        a_ps = products(range(0, 4), A_BANKS, w1_tile, "a_ps")
+        late_loads(4)
         damped(a_ps, 0)
         damped(a_ps, 1)
         prepare_w3(0, 0)
         quantise_h(0)
-        y_first = biased(0, 0, 2, "y_first")
+        y_first = projection(0, 0, 2)
         prepare_w3(1, 1)
         damped(a_ps, 2)
         damped(a_ps, 3)
+        weighted_first = held([P, GROUP], F32, "weighted_first")
+        nc.vector.scalar_tensor_tensor(weighted_first[:], y_first[:], by_sb[:, 0:1], weights(0), ALU.add, ALU.mult)
         prepare_w3(2, 2)
         quantise_h(1)
-        y_second = projection(0, 1, 3)
-        weighted_second = held([P, GROUP], F32, "weighted_second")
-        nc.vector.scalar_tensor_tensor(
-            weighted_second[:], y_second[:], by_sb[:, 1:2], weights(0), ALU.add, ALU.mult
-        )
-        scatter_product(0, 0, y_first)
-        nc.vector.tensor_copy(places(0, 1), weighted_second[:])
-        copied = ((0, 2, 4), (1, 0, 5), (1, 1, 2))
-        y_copied = [biased(group, n, bank) for group, n, bank in copied]
-        weighted = held([P, 3, GROUP], F32, "weighted", "y_first")
-        for k, (group, n, bank) in enumerate(copied):
-            nc.gpsimd.tensor_tensor(weighted[:, k, :], y_copied[k][:], weights(group), ALU.mult)
-            nc.vector.tensor_copy(places(group, n), weighted[:, k, :])
-        late_pair(4)
-        damped(a_ps, 4)
-        damped(a_ps, 5)
+        nc.vector.tensor_copy(places(0, 0), weighted_first[:])
+        y_second = biased(0, 1, 3)
+        y_third = biased(0, 2, 0)
+        y_fourth = biased(1, 0, 1)
+        weighted = held([P, 3, GROUP], F32, "weighted", "h_bf1")
+        scatter_copy(0, 1, y_second, weighted[:, 0, :])
+        scatter_copy(0, 2, y_third, weighted[:, 1, :])
+        scatter_copy(1, 0, y_fourth, weighted[:, 2, :])
+        root_of(4)
+        late_signal(4)
+        square_of(4)
+        damped_full(4)
+        y_fifth = biased(1, 1, 2)
+        weighted_fifth = held([P, GROUP], F32, "weighted_fifth", "damp4")
+        scatter_copy(1, 1, y_fifth, weighted_fifth[:])
+        root_of(5)
+        late_signal(5)
+        square_of(5)
+        damped_full(5)
+        y_sixth = biased(1, 2, 3)
+        late_loads(6)
+        rounded_h(4)
+        root_of(6)
+        rounded_h(5)
         quantise_h(2)
-        y_held = biased(1, 2, 3)
-        weighted_held = held([P, GROUP], F32, "weighted_held", "damp5")
-        nc.gpsimd.tensor_tensor(weighted_held[:], y_held[:], weights(1), ALU.mult)
-        nc.vector.tensor_copy(places(1, 2), weighted_held[:])
-        late_pair(6)
-        damped(a_ps, 6)
+        weighted_sixth = held([P, GROUP], F32, "weighted_sixth", "h_full5")
+        scatter_copy(1, 2, y_sixth, weighted_sixth[:])
+        late_signal(6)
+        square_of(6)
+        damped_full(6, "h_bf2")
+        root_of(7)
+        late_signal(7)
+        square_of(7)
+        y_seventh = biased(2, 0, 0, offset=ROOT_LAST_AT - KIB + LAP)
+        rounded_h(6)
         damped(a_ps, 7)
-        scatter_product(2, 0, biased(2, 0, 4, "root7"))
+        scatter_product(2, 0, y_seventh)
         quantise_h(3)
-        scatter_product(2, 1, biased(2, 1, 5, "damp7"))
+        scatter_product(2, 1, biased(2, 1, 1, "damp7"))
         scatter_product(3, 0, biased(3, 0, 2))
         scatter_product(3, 1, biased(3, 1, 3))
-        scatter_product(2, 2, biased(2, 2, 4, groups=2), groups=2)
+        scatter_product(2, 2, biased(2, 2, 0, groups=2), groups=2)

@@ -28,9 +28,10 @@ A_BANKS = (4, 5, 6, 7, 4, 5, 6, 7)
 ON_GPSIMD = (4, 5, 6)
 KIB = 1024
 LAP = 64
-TAB_AT = (20 * KIB, 36 * KIB, 0)
-TAB_SC_AT = 15 * KIB
-W2_SC_AT = 16 * KIB
+TAB_AT = (19 * KIB, 36 * KIB, 80 * KIB)
+TAB_SC_AT = 95 * KIB
+W2_SC_AT = 96 * KIB
+CACHE_AT = (0, 99 * KIB - LAP, 11 * KIB + LAP)
 W1_AT = (20 * KIB, 28 * KIB, 36 * KIB)
 W3_AT = 44 * KIB
 BY_AT = 50 * KIB
@@ -75,13 +76,15 @@ def tile_list_predicate_damped_store_kernel(
 
         nc.vector.memset(warm_in[:], 1.0)
         nc.scalar.activation(warm_out[:], warm_in[:], ACT.Abs_reciprocal_sqrt)
-        nc.gpsimd.memset(tab_sc[32:64, :], 0)
-        nc.gpsimd.memset(tab_sc[64:112, :], 0)
-        cache = [held([P, T2], F32, "cache%d" % n) for n in range(N // P)]
-        for zeroed in cache:
-            nc.gpsimd.memset(zeroed[:], 0.0)
+        cache = [placed([P, T2], F32, "cache%d" % n, CACHE_AT[n]) for n in range(N // P)]
+        nc.gpsimd.memset(cache[0][:, 0:GROUP], 0.0)
+        warm_product = held([P, CHUNK], F32, "warm_product")
+        nc.gpsimd.tensor_tensor(warm_product[:], cache[0][:, 0:CHUNK], cache[0][:, CHUNK:GROUP], ALU.mult)
+        nc.vector.memset(tab_sc[32:64, :], 0)
+        nc.vector.memset(tab_sc[64:112, :], 0)
         for a in range(PASSES):
             nc.vector.memset(v_sc[a][:], 0)
+        nc.vector.memset(cache[0][:, GROUP:], 0.0)
 
         def load_w1(a):
             rows = w1[512 * a : 512 * (a + 1), :].rearrange("(p j) c -> p j c", j=4)
@@ -124,7 +127,9 @@ def tile_list_predicate_damped_store_kernel(
                 v_halves[a, (first + c) // HALF] = gathered[:, c : c + HALF]
 
         nc.vector.memset(w2_sc[:], 0)
+        nc.vector.memset(cache[1][:], 0.0)
         gather_words(0, 0, S)
+        nc.vector.memset(cache[2][:], 0.0)
         load_w1(0)
         load_w1(1)
         nc.vector.tensor_copy(

@@ -25,7 +25,7 @@ SC_BASE = (0, 16, 112)
 GROUP = 256
 B_BANKS = (0, 1, 2, 3, 0, 1, 6, 7)
 A_BANKS = (4, 5, 6, 7, 4, 5, 6, 7)
-ON_GPSIMD = (4, 5, 6)
+ON_GPSIMD = (4, 5)
 KIB = 1024
 LAP = 64
 TAB_AT = (19 * KIB, 36 * KIB, 80 * KIB)
@@ -80,10 +80,10 @@ def tile_list_predicate_damped_store_kernel(
         nc.gpsimd.memset(cache[0][:, 0:GROUP], 0.0)
         warm_product = held([P, CHUNK], F32, "warm_product")
         nc.gpsimd.tensor_tensor(warm_product[:], cache[0][:, 0:CHUNK], cache[0][:, CHUNK:GROUP], ALU.mult)
-        nc.vector.memset(tab_sc[32:64, :], 0)
-        nc.vector.memset(tab_sc[64:112, :], 0)
+        nc.gpsimd.memset(tab_sc[32:64, :], 0)
+        nc.gpsimd.memset(tab_sc[64:112, :], 0)
         for a in range(PASSES):
-            nc.vector.memset(v_sc[a][:], 0)
+            nc.gpsimd.memset(v_sc[a][:], 0)
         nc.vector.memset(cache[0][:, GROUP:], 0.0)
 
         def load_w1(a):
@@ -258,10 +258,8 @@ def tile_list_predicate_damped_store_kernel(
 
         def h_target(g):
             group, u = divmod(g, 2)
-            if u == 0 and group < 3:
+            if u == 0:
                 h_bf[group] = held([P, GROUP, 4], BF16, "h_bf%d" % group)
-            elif u == 0:
-                h_bf[group] = placed([P, GROUP, 4], BF16, "h_bf%d" % group, ROOT_LAST_AT + KIB)
             return h_bf[group][:, u * CHUNK : (u + 1) * CHUNK, :]
 
         def damped(a_ps, g):
@@ -332,10 +330,6 @@ def tile_list_predicate_damped_store_kernel(
             if g in ON_GPSIMD:
                 nc.scalar.copy(a_sb[g][:], a_ps[g][:].rearrange("p t n -> p n t"))
 
-        def scatter_copy(group, n, y_sb, target):
-            nc.gpsimd.tensor_tensor(target, y_sb[:], weights(group), ALU.mult)
-            nc.vector.tensor_copy(places(group, n), target)
-
         b_ps = products(range(0, 4), B_BANKS, w2_tile, "b_ps")
         damping(b_ps, 0)
         damping(b_ps, 2)
@@ -360,39 +354,42 @@ def tile_list_predicate_damped_store_kernel(
         quantise_h(1)
         nc.vector.tensor_copy(places(0, 0), weighted_first[:])
         y_second = biased(0, 1, 3)
-        y_third = biased(0, 2, 0)
-        y_fourth = biased(1, 0, 1)
+        y_pair = held([P, 2, GROUP], F32, "y_pair")
+        for group, n in ((0, 2), (1, 0)):
+            nc.scalar.activation(y_pair[:, group, :], projection(group, n, group)[:], ACT.Identity, bias=by_sb[:, n : n + 1])
         weighted = held([P, 3, GROUP], F32, "weighted", "h_bf1")
-        scatter_copy(0, 1, y_second, weighted[:, 0, :])
-        scatter_copy(0, 2, y_third, weighted[:, 1, :])
-        scatter_copy(1, 0, y_fourth, weighted[:, 2, :])
+        nc.gpsimd.tensor_tensor(weighted[:, 0, :], y_second[:], weights(0), ALU.mult)
+        nc.vector.tensor_copy(places(0, 1), weighted[:, 0, :])
+        nc.gpsimd.tensor_tensor(
+            weighted[:, 1:3, :].rearrange("p g n -> p (g n)"),
+            y_pair[:].rearrange("p g n -> p (g n)"),
+            weights(0, 2),
+            ALU.mult,
+        )
+        nc.vector.tensor_copy(places(0, 2), weighted[:, 1, :])
+        nc.vector.tensor_copy(places(1, 0), weighted[:, 2, :])
         root_of(4)
         late_signal(4)
         square_of(4)
         damped_full(4)
-        y_fifth = biased(1, 1, 2)
-        weighted_fifth = held([P, GROUP], F32, "weighted_fifth", "damp4")
-        scatter_copy(1, 1, y_fifth, weighted_fifth[:])
         root_of(5)
         late_signal(5)
         square_of(5)
         damped_full(5)
-        y_sixth = biased(1, 2, 3)
         late_loads(6)
         rounded_h(4)
         root_of(6)
+        scatter_product(1, 1, biased(1, 1, 2, "damp4"))
         rounded_h(5)
         quantise_h(2)
-        weighted_sixth = held([P, GROUP], F32, "weighted_sixth", "h_full5")
-        scatter_copy(1, 2, y_sixth, weighted_sixth[:])
+        scatter_product(1, 2, biased(1, 2, 3, "h_full5"))
         late_signal(6)
         square_of(6)
-        damped_full(6, "h_bf2")
         root_of(7)
         late_signal(7)
         square_of(7)
         y_seventh = biased(2, 0, 0, offset=ROOT_LAST_AT - KIB + LAP)
-        rounded_h(6)
+        damped(a_ps, 6)
         damped(a_ps, 7)
         scatter_product(2, 0, y_seventh)
         quantise_h(3)

@@ -28,11 +28,12 @@ A_BANKS = (4, 5, 6, 7, 4, 5, 6, 7)
 ON_GPSIMD = (4, 5)
 KIB = 1024
 LAP = 64
-TAB_AT = (19 * KIB, 36 * KIB, 80 * KIB)
+TAB_AT = (8 * KIB, 36 * KIB, 80 * KIB)
 TAB_SC_AT = 95 * KIB
 W2_SC_AT = 96 * KIB
-CACHE_AT = (0, 99 * KIB - LAP, 11 * KIB + LAP)
-W1_AT = (20 * KIB, 28 * KIB, 36 * KIB)
+W2_SC_RAW_AT = 27 * KIB
+CACHE_AT = (0, 99 * KIB - LAP, 28 * KIB)
+W1_AT = (8 * KIB, 16 * KIB, 36 * KIB)
 W3_AT = 44 * KIB
 BY_AT = 50 * KIB
 WGO_AT = 50 * KIB + LAP
@@ -61,7 +62,7 @@ def tile_list_predicate_damped_store_kernel(
         tab = [placed([P, T], I32, "tab%d" % a, TAB_AT[a]) for a in range(PASSES)]
         tab_sc = placed([P, T // 4], I32, "tab_sc", TAB_SC_AT)
         w2_raw = held([P, PASSES, H // 2], I32, "w2_raw")
-        w2_sc_raw = held([P, PASSES, H // 4], I32, "w2_sc_raw")
+        w2_sc_raw = placed([P, PASSES, H // 4], I32, "w2_sc_raw", W2_SC_RAW_AT)
         w1_raw = [placed([P, 4, H], F32, "w1_raw%d" % a, W1_AT[a]) for a in range(PASSES - 1)]
         w1_last = [placed([P, 2, H], F32, "w1_last%d" % u, W1_AT[PASSES - 1] + 4 * KIB * u) for u in range(2)]
         v_packed = held([P, S // 4], I32, "v_packed")
@@ -129,7 +130,6 @@ def tile_list_predicate_damped_store_kernel(
         nc.vector.memset(w2_sc[:], 0)
         nc.vector.memset(cache[1][:], 0.0)
         gather_words(0, 0, S)
-        nc.vector.memset(cache[2][:], 0.0)
         load_w1(0)
         load_w1(1)
         nc.vector.tensor_copy(
@@ -142,6 +142,7 @@ def tile_list_predicate_damped_store_kernel(
                 w2_sc[rows].rearrange("p a (t q w) -> p a t q w", t=4, w=2),
                 w2_sc_raw[rows].rearrange("p a (q t w) -> p a t q w", t=4, w=2),
             )
+        nc.vector.memset(cache[2][:], 0.0)
         gather_words(1, 0, S)
         load_w1(2)
         w3_rows = w3.rearrange("(q t i) n -> t q i n", t=4, i=8)
@@ -246,8 +247,8 @@ def tile_list_predicate_damped_store_kernel(
                 square_of(g + 1)
 
         h_bf = {}
-        h_codes = held([P, S], U32, "h_codes")
-        h_sc = held([P, S], U8, "h_sc")
+        h_codes = [held([P, HALF], U32, "h_codes0"), placed([P, HALF], U32, "h_codes1", ROOT_LAST_AT)]
+        h_sc = [held([P, HALF], U8, "h_sc%d" % half) for half in range(2)]
         w3_codes = {}
         w3_sc = [held([P, P], U8, "w3_sc%d" % n) for n in range(N // P)]
         w3_bf = [placed([P, P, 4], BF16, "w3_bf%d" % n, ABS_AT[1] + n * KIB) for n in range(N // P)]
@@ -273,9 +274,10 @@ def tile_list_predicate_damped_store_kernel(
             nc.scalar.copy(h_target(g), h_full[g][:])
 
         def quantise_h(group):
-            cols = slice(GROUP * group, GROUP * (group + 1))
+            half, start = divmod(GROUP * group, HALF)
+            cols = slice(start, start + GROUP)
             nc.vector.quantize_mx(
-                h_codes[:, cols].bitcast(FP8X4), h_sc[:, cols], h_bf[group][:].rearrange("p n t -> p (n t)")
+                h_codes[half][:, cols].bitcast(FP8X4), h_sc[half][:, cols], h_bf[group][:].rearrange("p n t -> p (n t)")
             )
 
         def prepare_w3(n, after):
@@ -287,14 +289,15 @@ def tile_list_predicate_damped_store_kernel(
             )
 
         def projection(group, n, bank, groups=1):
-            cols = slice(GROUP * group, GROUP * (group + groups))
+            half, start = divmod(GROUP * group, HALF)
+            cols = slice(start, start + GROUP * groups)
             y_ps = psum.tile([P, GROUP * groups], F32, name="y_ps", tag="bank%d" % bank)
             nc.tensor.matmul_mx(
                 y_ps[:],
                 lhsT=w3_codes[n][:].bitcast(FP8X4),
                 lhsT_scale=w3_sc[n][:],
-                rhs=h_codes[:, cols].bitcast(FP8X4),
-                rhs_scale=h_sc[:, cols],
+                rhs=h_codes[half][:, cols].bitcast(FP8X4),
+                rhs_scale=h_sc[half][:, cols],
                 start=True,
                 stop=True,
             )
@@ -306,12 +309,9 @@ def tile_list_predicate_damped_store_kernel(
         def weights(group, groups=1):
             return wgo_sb[:, GROUP * group : GROUP * (group + groups)]
 
-        def biased(group, n, bank, tag=None, groups=1, offset=None):
+        def biased(group, n, bank, tag=None, groups=1):
             y_ps = projection(group, n, bank, groups)
-            if offset is None:
-                y_sb = held([P, GROUP * groups], F32, "y_sb%d_%d" % (group, n), tag)
-            else:
-                y_sb = placed([P, GROUP * groups], F32, "y_sb%d_%d" % (group, n), offset)
+            y_sb = held([P, GROUP * groups], F32, "y_sb%d_%d" % (group, n), tag)
             nc.scalar.activation(y_sb[:], y_ps[:], ACT.Identity, bias=by_sb[:, n : n + 1])
             return y_sb
 
@@ -377,23 +377,25 @@ def tile_list_predicate_damped_store_kernel(
         square_of(5)
         damped_full(5)
         late_loads(6)
-        rounded_h(4)
         root_of(6)
         scatter_product(1, 1, biased(1, 1, 2, "damp4"))
-        rounded_h(5)
-        quantise_h(2)
-        scatter_product(1, 2, biased(1, 2, 3, "h_full5"))
         late_signal(6)
         square_of(6)
         root_of(7)
+        rounded_h(4)
         late_signal(7)
         square_of(7)
-        y_seventh = biased(2, 0, 0, offset=ROOT_LAST_AT - KIB + LAP)
+        rounded_h(5)
         damped(a_ps, 6)
         damped(a_ps, 7)
-        scatter_product(2, 0, y_seventh)
+        quantise_h(2)
         quantise_h(3)
-        scatter_product(2, 1, biased(2, 1, 1, "damp7"))
-        scatter_product(3, 0, biased(3, 0, 2))
-        scatter_product(3, 1, biased(3, 1, 3))
-        scatter_product(2, 2, biased(2, 2, 0, groups=2), groups=2)
+        scatter_product(1, 2, biased(1, 2, 3, "damp6"))
+        y_wide = held([P, HALF], F32, "y_wide")
+        for u in range(2):
+            nc.scalar.activation(
+                y_wide[:, GROUP * u : GROUP * (u + 1)], projection(2 + u, 0, u)[:], ACT.Identity, bias=by_sb[:, 0:1]
+            )
+        scatter_product(2, 0, y_wide, groups=2)
+        for n in range(1, N // P):
+            scatter_product(2, n, biased(2, n, 1 + n, groups=2), groups=2)

@@ -24,8 +24,7 @@ CHUNKS = S // CHUNK
 SC_BASE = (0, 16, 112)
 GROUP = 256
 B_BANKS = (0, 1, 2, 3, 0, 1, 6, 7)
-A_BANKS = (4, 5, 6, 7, 4, 5, 6, 7)
-ON_GPSIMD = (4, 5)
+A_BANKS = (4, 5, 6, 7, 4, 5, 4, 5)
 KIB = 1024
 LAP = 64
 TAB_AT = (8 * KIB, 36 * KIB, 80 * KIB)
@@ -38,7 +37,6 @@ W3_AT = 44 * KIB
 BY_AT = 50 * KIB
 WGO_AT = 50 * KIB + LAP
 ABS_AT = (56 * KIB, 60 * KIB, 56 * KIB, 64 * KIB)
-ROOT_LAST_AT = 72 * KIB
 
 
 def tile_list_predicate_damped_store_kernel(
@@ -215,8 +213,8 @@ def tile_list_predicate_damped_store_kernel(
             return accs
 
         damp = {g: held([P, CHUNK, 4], F32, "damp%d" % g) for g in range(CHUNKS) if g != 3}
-
         sizes = {}
+        roots = {}
 
         def magnitudes(b_ps, g):
             size = placed([P, 2, CHUNK, 4], F32, "b_abs%d" % g, ABS_AT[g // 2])
@@ -224,12 +222,8 @@ def tile_list_predicate_damped_store_kernel(
                 nc.scalar.activation(size[:, u], b_ps[g + u][:].rearrange("p t n -> p n t"), ACT.Abs)
                 sizes[g + u] = size[:, u]
 
-        roots = {}
-
         def root_of(g):
-            if g == CHUNKS - 1:
-                roots[g] = placed([P, CHUNK, 4], F32, "root7", ROOT_LAST_AT)
-            elif g >= 4:
+            if g >= 4:
                 roots[g] = placed([P, CHUNK, 4], F32, "root%d" % g, W3_AT + 2 * KIB * (g % 2))
             else:
                 roots[g] = ring.tile([P, CHUNK, 4], F32, name="root")
@@ -238,47 +232,34 @@ def tile_list_predicate_damped_store_kernel(
         def square_of(g):
             nc.scalar.activation(damp[g][:], roots[g][:], ACT.Square)
 
-        def damping(b_ps, g):
-            magnitudes(b_ps, g)
-            root_of(g)
-            root_of(g + 1)
-            square_of(g)
-            if g == 0:
-                square_of(g + 1)
-
         h_bf = {}
-        h_codes = [held([P, HALF], U32, "h_codes0"), placed([P, HALF], U32, "h_codes1", ROOT_LAST_AT)]
-        h_sc = [held([P, HALF], U8, "h_sc%d" % half) for half in range(2)]
+        h_codes = {}
+        h_sc = [held([P, GROUP], U8, "h_sc%d" % group) for group in range(S // GROUP)]
         w3_codes = {}
         w3_sc = [held([P, P], U8, "w3_sc%d" % n) for n in range(N // P)]
         w3_bf = [placed([P, P, 4], BF16, "w3_bf%d" % n, ABS_AT[1] + n * KIB) for n in range(N // P)]
+        a_sb = {g: held([P, CHUNK * 4], F32, "a_sb%d" % g) for g in range(4, CHUNKS)}
 
-        a_sb = {g: held([P, CHUNK, 4], F32, "a_sb%d" % g) for g in ON_GPSIMD}
-
-        h_full = {}
-
-        def h_target(g):
+        def h_target(g, tag=None):
             group, u = divmod(g, 2)
             if u == 0:
-                h_bf[group] = held([P, GROUP, 4], BF16, "h_bf%d" % group)
-            return h_bf[group][:, u * CHUNK : (u + 1) * CHUNK, :]
+                h_bf[group] = held([P, GROUP * 4], BF16, "h_bf%d" % group, tag)
+            return h_bf[group][:, u * CHUNK * 4 : (u + 1) * CHUNK * 4]
 
         def damped(a_ps, g):
-            nc.vector.tensor_tensor(h_target(g), a_ps[g][:].rearrange("p t n -> p n t"), damp[g][:], ALU.mult)
-
-        def damped_full(g, tag=None):
-            h_full[g] = held([P, CHUNK, 4], F32, "h_full%d" % g, tag)
-            nc.gpsimd.tensor_tensor(h_full[g][:], a_sb[g][:], damp[g][:], ALU.mult)
-
-        def rounded_h(g):
-            nc.scalar.copy(h_target(g), h_full[g][:])
-
-        def quantise_h(group):
-            half, start = divmod(GROUP * group, HALF)
-            cols = slice(start, start + GROUP)
-            nc.vector.quantize_mx(
-                h_codes[half][:, cols].bitcast(FP8X4), h_sc[half][:, cols], h_bf[group][:].rearrange("p n t -> p (n t)")
+            nc.vector.tensor_tensor(
+                h_target(g).rearrange("p (n t) -> p n t", t=4),
+                a_ps[g][:].rearrange("p t n -> p n t"),
+                damp[g][:],
+                ALU.mult,
             )
+
+        def damped_aside(g, tag=None):
+            nc.gpsimd.tensor_tensor(h_target(g, tag), a_sb[g][:], damp[g][:].rearrange("p n t -> p (n t)"), ALU.mult)
+
+        def quantise_h(group, tag=None):
+            h_codes[group] = held([P, GROUP], U32, "h_codes%d" % group, tag)
+            nc.vector.quantize_mx(h_codes[group][:].bitcast(FP8X4), h_sc[group][:], h_bf[group][:])
 
         def prepare_w3(n, after):
             cols = slice(P * n, P * (n + 1))
@@ -289,19 +270,18 @@ def tile_list_predicate_damped_store_kernel(
             )
 
         def projection(group, n, bank, groups=1):
-            half, start = divmod(GROUP * group, HALF)
-            cols = slice(start, start + GROUP * groups)
-            y_ps = psum.tile([P, GROUP * groups], F32, name="y_ps", tag="bank%d" % bank)
-            nc.tensor.matmul_mx(
-                y_ps[:],
-                lhsT=w3_codes[n][:].bitcast(FP8X4),
-                lhsT_scale=w3_sc[n][:],
-                rhs=h_codes[half][:, cols].bitcast(FP8X4),
-                rhs_scale=h_sc[half][:, cols],
-                start=True,
-                stop=True,
-            )
-            return y_ps
+            y_ps = psum.tile([P, groups, GROUP], F32, name="y_ps", tag="bank%d" % bank)
+            for u in range(groups):
+                nc.tensor.matmul_mx(
+                    y_ps[:, u, :],
+                    lhsT=w3_codes[n][:].bitcast(FP8X4),
+                    lhsT_scale=w3_sc[n][:],
+                    rhs=h_codes[group + u][:].bitcast(FP8X4),
+                    rhs_scale=h_sc[group + u][:],
+                    start=True,
+                    stop=True,
+                )
+            return y_ps[:].rearrange("p g n -> p (g n)")
 
         def places(group, n, groups=1):
             return cache[n][:].indirect(idx2[:, GROUP * group // 16 : GROUP * (group + groups) // 16])
@@ -309,14 +289,11 @@ def tile_list_predicate_damped_store_kernel(
         def weights(group, groups=1):
             return wgo_sb[:, GROUP * group : GROUP * (group + groups)]
 
-        def biased(group, n, bank, tag=None, groups=1):
-            y_ps = projection(group, n, bank, groups)
-            y_sb = held([P, GROUP * groups], F32, "y_sb%d_%d" % (group, n), tag)
-            nc.scalar.activation(y_sb[:], y_ps[:], ACT.Identity, bias=by_sb[:, n : n + 1])
-            return y_sb
+        def biased(target, group, n, bank, groups=1):
+            nc.scalar.activation(target, projection(group, n, bank, groups), ACT.Identity, bias=by_sb[:, n : n + 1])
 
         def scatter_product(group, n, y_sb, groups=1):
-            nc.vector.tensor_tensor(places(group, n, groups), y_sb[:], weights(group, groups), ALU.mult)
+            nc.vector.tensor_tensor(places(group, n, groups), y_sb, weights(group, groups), ALU.mult)
             if group + groups == S // GROUP:
                 nc.sync.dma_start(out[P * n : P * (n + 1), :], cache[n][:])
 
@@ -325,14 +302,20 @@ def tile_list_predicate_damped_store_kernel(
                 b_ps.update(products([g], B_BANKS, w2_tile, "b_ps"))
             magnitudes(b_ps, pair)
 
-        def late_signal(g):
+        def late_factors(g):
+            root_of(g)
             a_ps.update(products([g], A_BANKS, w1_tile, "a_ps"))
-            if g in ON_GPSIMD:
-                nc.scalar.copy(a_sb[g][:], a_ps[g][:].rearrange("p t n -> p n t"))
+            nc.scalar.copy(a_sb[g][:].rearrange("p (n t) -> p n t", t=4), a_ps[g][:].rearrange("p t n -> p n t"))
+            square_of(g)
 
         b_ps = products(range(0, 4), B_BANKS, w2_tile, "b_ps")
-        damping(b_ps, 0)
-        damping(b_ps, 2)
+        for g in (0, 2):
+            magnitudes(b_ps, g)
+            root_of(g)
+            root_of(g + 1)
+            square_of(g)
+            if g == 0:
+                square_of(g + 1)
         prepare_w1(0, 2)
         prepare_w1(1, 2)
         prepare_w1(2, 4)
@@ -349,17 +332,20 @@ def tile_list_predicate_damped_store_kernel(
         damped(a_ps, 2)
         damped(a_ps, 3)
         weighted_first = held([P, GROUP], F32, "weighted_first")
-        nc.vector.scalar_tensor_tensor(weighted_first[:], y_first[:], by_sb[:, 0:1], weights(0), ALU.add, ALU.mult)
+        nc.vector.scalar_tensor_tensor(weighted_first[:], y_first, by_sb[:, 0:1], weights(0), ALU.add, ALU.mult)
         prepare_w3(2, 2)
         quantise_h(1)
         nc.vector.tensor_copy(places(0, 0), weighted_first[:])
-        y_second = biased(0, 1, 3)
-        y_pair = held([P, 2, GROUP], F32, "y_pair")
-        for group, n in ((0, 2), (1, 0)):
-            nc.scalar.activation(y_pair[:, group, :], projection(group, n, group)[:], ACT.Identity, bias=by_sb[:, n : n + 1])
+
+        y_second = held([P, GROUP], F32, "y_second")
+        biased(y_second[:], 0, 1, 3)
         weighted = held([P, 3, GROUP], F32, "weighted", "h_bf1")
         nc.gpsimd.tensor_tensor(weighted[:, 0, :], y_second[:], weights(0), ALU.mult)
         nc.vector.tensor_copy(places(0, 1), weighted[:, 0, :])
+        late_factors(4)
+        y_pair = held([P, 2, GROUP], F32, "y_pair", "stage")
+        biased(y_pair[:, 0, :], 0, 2, 0)
+        biased(y_pair[:, 1, :], 1, 0, 1)
         nc.gpsimd.tensor_tensor(
             weighted[:, 1:3, :].rearrange("p g n -> p (g n)"),
             y_pair[:].rearrange("p g n -> p (g n)"),
@@ -368,34 +354,37 @@ def tile_list_predicate_damped_store_kernel(
         )
         nc.vector.tensor_copy(places(0, 2), weighted[:, 1, :])
         nc.vector.tensor_copy(places(1, 0), weighted[:, 2, :])
-        root_of(4)
-        late_signal(4)
-        square_of(4)
-        damped_full(4)
-        root_of(5)
-        late_signal(5)
-        square_of(5)
-        damped_full(5)
-        late_loads(6)
-        root_of(6)
-        scatter_product(1, 1, biased(1, 1, 2, "damp4"))
-        late_signal(6)
-        square_of(6)
-        root_of(7)
-        rounded_h(4)
-        late_signal(7)
-        square_of(7)
-        rounded_h(5)
-        damped(a_ps, 6)
-        damped(a_ps, 7)
+        damped_aside(4, "stage")
+        late_factors(5)
+        damped_aside(5)
         quantise_h(2)
+        y_rest = held([P, 2, GROUP], F32, "y_rest")
+        biased(y_rest[:, 0, :], 1, 1, 2)
+        biased(y_rest[:, 1, :], 1, 2, 3)
+        weighted_rest = held([P, 2, GROUP], F32, "weighted_rest", "a_sb5")
+        nc.gpsimd.tensor_tensor(
+            weighted_rest[:], y_rest[:], weights(1).unsqueeze(1).to_broadcast([P, 2, GROUP]), ALU.mult
+        )
+        nc.vector.tensor_copy(places(1, 1), weighted_rest[:, 0, :])
+        nc.vector.tensor_copy(places(1, 2), weighted_rest[:, 1, :])
+        late_loads(6)
+        late_factors(6)
+        damped_aside(6, "stage")
+        late_factors(7)
+        y_third = h_bf[3][:, CHUNK * 4 :].bitcast(F32)
+        biased(y_third, 2, 0, 0)
+        weighted_third = held([P, GROUP], F32, "weighted_third")
+        nc.gpsimd.tensor_tensor(weighted_third[:], y_third, weights(2), ALU.mult)
+        nc.vector.tensor_copy(places(2, 0), weighted_third[:])
+        damped_aside(7)
         quantise_h(3)
-        scatter_product(1, 2, biased(1, 2, 3, "damp6"))
+        y_cover = held([P, GROUP], F32, "y_cover", "damp7")
+        biased(y_cover[:], 2, 1, 1)
+        scatter_product(2, 1, y_cover[:])
+        for n in range(2):
+            y_last = held([P, GROUP], F32, "y_last%d" % n)
+            biased(y_last[:], 3, n, 2 + n)
+            scatter_product(3, n, y_last[:])
         y_wide = held([P, HALF], F32, "y_wide")
-        for u in range(2):
-            nc.scalar.activation(
-                y_wide[:, GROUP * u : GROUP * (u + 1)], projection(2 + u, 0, u)[:], ACT.Identity, bias=by_sb[:, 0:1]
-            )
-        scatter_product(2, 0, y_wide, groups=2)
-        for n in range(1, N // P):
-            scatter_product(2, n, biased(2, n, 1 + n, groups=2), groups=2)
+        biased(y_wide[:], 2, 2, 6, groups=2)
+        scatter_product(2, 2, y_wide[:], groups=2)

@@ -212,7 +212,7 @@ def tile_list_predicate_damped_store_kernel(
                     product_pass(accs[g], g, a, stationary)
             return accs
 
-        damp = {g: held([P, CHUNK, 4], F32, "damp%d" % g) for g in range(CHUNKS) if g != 3}
+        damp = {g: held([P, CHUNK, 4], F32, "damp%d" % g) for g in range(CHUNKS) if g not in (2, 3)}
         sizes = {}
         roots = {}
 
@@ -240,10 +240,10 @@ def tile_list_predicate_damped_store_kernel(
         w3_bf = [placed([P, P, 4], BF16, "w3_bf%d" % n, ABS_AT[1] + n * KIB) for n in range(N // P)]
         a_sb = {g: held([P, CHUNK * 4], F32, "a_sb%d" % g) for g in range(4, CHUNKS)}
 
-        def h_target(g, tag=None):
+        def h_target(g, tag=None, spare=0):
             group, u = divmod(g, 2)
-            if u == 0:
-                h_bf[group] = held([P, GROUP * 4], BF16, "h_bf%d" % group, tag)
+            if group not in h_bf:
+                h_bf[group] = held([P, GROUP * (4 + spare)], BF16, "h_bf%d" % group, tag)
             return h_bf[group][:, u * CHUNK * 4 : (u + 1) * CHUNK * 4]
 
         def damped(a_ps, g):
@@ -259,11 +259,11 @@ def tile_list_predicate_damped_store_kernel(
 
         def quantise_h(group, tag=None):
             h_codes[group] = held([P, GROUP], U32, "h_codes%d" % group, tag)
-            nc.vector.quantize_mx(h_codes[group][:].bitcast(FP8X4), h_sc[group][:], h_bf[group][:])
+            nc.vector.quantize_mx(h_codes[group][:].bitcast(FP8X4), h_sc[group][:], h_bf[group][:, 0 : GROUP * 4])
 
         def prepare_w3(n, after):
             cols = slice(P * n, P * (n + 1))
-            w3_codes[n] = held([P, P], U32, "w3_codes%d" % n, "damp%d" % after)
+            w3_codes[n] = held([P, P], U32, "w3_codes%d" % n, after)
             nc.scalar.copy(w3_bf[n][:], w3_raw[:, :, cols].rearrange("p t n -> p n t"))
             nc.vector.quantize_mx(
                 w3_codes[n][:].bitcast(FP8X4), w3_sc[n][:], w3_bf[n][:].rearrange("p n t -> p (n t)")
@@ -303,7 +303,8 @@ def tile_list_predicate_damped_store_kernel(
             magnitudes(b_ps, pair)
 
         def late_factors(g):
-            root_of(g)
+            if g not in roots:
+                root_of(g)
             a_ps.update(products([g], A_BANKS, w1_tile, "a_ps"))
             nc.scalar.copy(a_sb[g][:].rearrange("p (n t) -> p n t", t=4), a_ps[g][:].rearrange("p t n -> p n t"))
             square_of(g)
@@ -313,30 +314,33 @@ def tile_list_predicate_damped_store_kernel(
             magnitudes(b_ps, g)
             root_of(g)
             root_of(g + 1)
-            square_of(g)
             if g == 0:
+                square_of(g)
                 square_of(g + 1)
         prepare_w1(0, 2)
         prepare_w1(1, 2)
         prepare_w1(2, 4)
+        damp[2] = held([P, CHUNK, 4], F32, "damp2", "w1_bf2_0")
+        nc.vector.tensor_tensor(damp[2][:], roots[2][:], roots[2][:], ALU.mult)
         damp[3] = held([P, CHUNK, 4], F32, "damp3", "w1_bf2_1")
         nc.gpsimd.tensor_tensor(damp[3][:], roots[3][:], roots[3][:], ALU.mult)
         a_ps = products(range(0, 4), A_BANKS, w1_tile, "a_ps")
         late_loads(4)
         damped(a_ps, 0)
         damped(a_ps, 1)
-        prepare_w3(0, 0)
+        prepare_w3(0, "damp0")
         quantise_h(0)
         y_first = projection(0, 0, 2)
-        prepare_w3(1, 1)
+        prepare_w3(1, "damp1")
         damped(a_ps, 2)
         damped(a_ps, 3)
         weighted_first = held([P, GROUP], F32, "weighted_first")
         nc.vector.scalar_tensor_tensor(weighted_first[:], y_first, by_sb[:, 0:1], weights(0), ALU.add, ALU.mult)
-        prepare_w3(2, 2)
+        prepare_w3(2, "w1_bf2_0")
         quantise_h(1)
         nc.vector.tensor_copy(places(0, 0), weighted_first[:])
 
+        root_of(4)
         y_second = held([P, GROUP], F32, "y_second")
         biased(y_second[:], 0, 1, 3)
         weighted = held([P, 3, GROUP], F32, "weighted", "h_bf1")
@@ -361,17 +365,18 @@ def tile_list_predicate_damped_store_kernel(
         y_rest = held([P, 2, GROUP], F32, "y_rest")
         biased(y_rest[:, 0, :], 1, 1, 2)
         biased(y_rest[:, 1, :], 1, 2, 3)
-        weighted_rest = held([P, 2, GROUP], F32, "weighted_rest", "a_sb5")
-        nc.gpsimd.tensor_tensor(
-            weighted_rest[:], y_rest[:], weights(1).unsqueeze(1).to_broadcast([P, 2, GROUP]), ALU.mult
-        )
-        nc.vector.tensor_copy(places(1, 1), weighted_rest[:, 0, :])
-        nc.vector.tensor_copy(places(1, 2), weighted_rest[:, 1, :])
+        weighted_fifth = held([P, GROUP], F32, "weighted_fifth", "a_sb5")
+        nc.gpsimd.tensor_tensor(weighted_fifth[:], y_rest[:, 0, :], weights(1), ALU.mult)
+        nc.vector.tensor_copy(places(1, 1), weighted_fifth[:])
+        h_target(6, "stage", spare=2)
+        weighted_sixth = h_bf[3][:, GROUP * 4 :].bitcast(F32)
+        nc.gpsimd.tensor_tensor(weighted_sixth, y_rest[:, 1, :], weights(1), ALU.mult)
+        nc.vector.tensor_copy(places(1, 2), weighted_sixth)
         late_loads(6)
         late_factors(6)
-        damped_aside(6, "stage")
+        damped_aside(6)
         late_factors(7)
-        y_third = h_bf[3][:, CHUNK * 4 :].bitcast(F32)
+        y_third = h_bf[3][:, CHUNK * 4 : GROUP * 4].bitcast(F32)
         biased(y_third, 2, 0, 0)
         weighted_third = held([P, GROUP], F32, "weighted_third")
         nc.gpsimd.tensor_tensor(weighted_third[:], y_third, weights(2), ALU.mult)

from contextlib import ExitStack

import concourse.mybir as mybir

K, H, N, T, S, T2 = 1536, 512, 384, 4096, 1024, 2048
P = 128
PASSES = K // 512
FLOPS = 2 * (2 * K * H * S + H * N * S)

F32 = mybir.dt.float32
BF16 = mybir.dt.bfloat16
I32 = mybir.dt.int32
U32 = mybir.dt.uint32
U16 = mybir.dt.uint16
U8 = mybir.dt.uint8
FP8X4 = mybir.dt.float8_e4m3fn_x4
FP4X4 = mybir.dt.float4_e2m1fn_x4
ACT = mybir.ActivationFunctionType
ALU = mybir.AluOpType

CHUNK = 128
HALF = 512
CHUNKS = S // CHUNK
SC_BASE = (0, 16, 112)
GROUP = 256
B_BANKS = (0, 1, 2, 3, 0, 1, 6, 7)
A_BANKS = (4, 5, 6, 7, 4, 5, 4, 5)
KIB = 1024
LAP = 64
TAB_AT = (8 * KIB, 36 * KIB, 80 * KIB)
TAB_SC_AT = 95 * KIB
W2_SC_AT = 96 * KIB
W2_SC_RAW_AT = 27 * KIB
CACHE_AT = (0, 99 * KIB - LAP, 28 * KIB)
W1_AT = (8 * KIB, 16 * KIB, 36 * KIB)
W3_AT = 44 * KIB
BY_AT = 50 * KIB
WGO_AT = 50 * KIB + LAP
ABS_AT = (56 * KIB, 60 * KIB, 56 * KIB, 64 * KIB)


def tile_list_predicate_damped_store_kernel(
    tc, tab_words, tab_scales, offs, w1, w2_words, w2_scales, w3, by, wgo, offs2, out
):
    nc = tc.nc
    with ExitStack() as ctx:
        keep = ctx.enter_context(tc.tile_pool(name="keep", bufs=1))
        shared = ctx.enter_context(tc.tile_pool(name="shared", bufs=1))
        ring = ctx.enter_context(tc.tile_pool(name="ring", bufs=2))
        psum = ctx.enter_context(tc.psum_pool(name="psum", bufs=1))

        def held(shape, dtype, name, tag=None):
            return keep.tile(shape, dtype, name=name, tag=tag or name, align_bytes=64)

        def placed(shape, dtype, name, offset):
            return shared.tile(shape, dtype, name=name, offset=offset, align_bytes=64)

        idx = keep.tile([P, S // 16], U16, name="idx")
        idx2 = keep.tile([P, S // 16], U16, name="idx2")
        tab = [placed([P, T], I32, "tab%d" % a, TAB_AT[a]) for a in range(PASSES)]
        tab_sc = placed([P, T // 4], I32, "tab_sc", TAB_SC_AT)
        w2_raw = held([P, PASSES, H // 2], I32, "w2_raw")
        w2_sc_raw = placed([P, PASSES, H // 4], I32, "w2_sc_raw", W2_SC_RAW_AT)
        w1_raw = [placed([P, 4, H], F32, "w1_raw%d" % a, W1_AT[a]) for a in range(PASSES - 1)]
        w1_last = [placed([P, 2, H], F32, "w1_last%d" % u, W1_AT[PASSES - 1] + 4 * KIB * u) for u in range(2)]
        v_packed = held([P, S // 4], I32, "v_packed")
        w3_raw = placed([P, 4, N], F32, "w3_raw", W3_AT)
        wgo_sb = placed([P, S], F32, "wgo_sb", WGO_AT)
        w2_codes = held([P, PASSES, H // 2], I32, "w2_codes")
        w2_sc = placed([P, PASSES, H // 4], I32, "w2_sc", W2_SC_AT)
        by_sb = placed([P, N // P], F32, "by_sb", BY_AT)
        v_sc = [held([P, S // 4], I32, "v_sc%d" % a) for a in range(PASSES)]
        warm_in = held([P, 1], F32, "warm_in")
        warm_out = held([P, 1], F32, "warm_out")

        nc.vector.memset(warm_in[:], 1.0)
        nc.scalar.activation(warm_out[:], warm_in[:], ACT.Abs_reciprocal_sqrt)
        cache = [placed([P, T2], F32, "cache%d" % n, CACHE_AT[n]) for n in range(N // P)]
        nc.gpsimd.memset(cache[0][:, 0:GROUP], 0.0)
        warm_product = held([P, CHUNK], F32, "warm_product")
        nc.gpsimd.tensor_tensor(warm_product[:], cache[0][:, 0:CHUNK], cache[0][:, CHUNK:GROUP], ALU.mult)
        nc.gpsimd.memset(tab_sc[32:64, :], 0)
        nc.gpsimd.memset(tab_sc[64:112, :], 0)
        for a in range(PASSES):
            nc.gpsimd.memset(v_sc[a][:], 0)
        nc.vector.memset(cache[0][:, GROUP:], 0.0)

        def load_w1(a):
            rows = w1[512 * a : 512 * (a + 1), :].rearrange("(p j) c -> p j c", j=4)
            if a < PASSES - 1:
                nc.sync.dma_start(w1_raw[a][:], rows)
            else:
                for u in range(2):
                    nc.sync.dma_start(w1_last[u][:], rows[:, 2 * u : 2 * u + 2, :])

        def load_table(a):
            nc.sync.dma_start(tab[a][:], tab_words[a].rearrange("p t i -> p (t i)").bitcast(I32))

        nc.sync.dma_start(idx[:], offs)
        nc.sync.dma_start(tab_sc[0:32, :], tab_scales[0:2].rearrange("a q t -> (a q) t").bitcast(I32))
        nc.sync.dma_start(tab_sc[112:128, :], tab_scales[2].bitcast(I32))
        nc.sync.dma_start(w2_raw[:], w2_words.rearrange("a p b -> p a b").bitcast(I32))
        load_table(0)
        for quad in range(4):
            nc.sync.dma_start(
                w2_sc_raw[32 * quad : 32 * quad + 4, :, :],
                w2_scales[:, 4 * quad : 4 * quad + 4, :].rearrange("a r c -> r a c").bitcast(I32),
            )
        nc.sync.dma_start(idx2[:], offs2)
        load_table(1)

        nc.vector.tensor_copy(v_packed[:].bitcast(U8), tab_sc[:].bitcast(U8).indirect(idx[:]))
        moves = [(a, r) for a in range(PASSES) for r in range(4)]
        for k, (a, r) in enumerate(moves):
            if k == len(moves) // 2:
                load_table(2)
            nc.sync.dma_start(v_sc[a][r:P:32, :], v_packed[SC_BASE[a] + r : SC_BASE[a] + 16 : 4, :])

        v_halves = {}

        def gather_words(a, first, width):
            gathered = held([P, width], I32, "v_codes%d_%d" % (a, first))
            cols = slice(first // 16, (first + width) // 16)
            nc.vector.tensor_copy(gathered[:].bitcast(U32), tab[a][:].bitcast(U32).indirect(idx[:, cols]))
            for c in range(0, width, HALF):
                v_halves[a, (first + c) // HALF] = gathered[:, c : c + HALF]

        nc.vector.memset(w2_sc[:], 0)
        nc.vector.memset(cache[1][:], 0.0)
        gather_words(0, 0, S)
        load_w1(0)
        load_w1(1)
        nc.vector.tensor_copy(
            w2_codes[:].rearrange("p a (t q w) -> p a t q w", t=4, w=4),
            w2_raw[:].rearrange("p a (q t w) -> p a t q w", t=4, w=4),
        )
        for quad in range(4):
            rows = slice(32 * quad, 32 * quad + 4)
            nc.vector.tensor_copy(
                w2_sc[rows].rearrange("p a (t q w) -> p a t q w", t=4, w=2),
                w2_sc_raw[rows].rearrange("p a (q t w) -> p a t q w", t=4, w=2),
            )
        nc.vector.memset(cache[2][:], 0.0)
        gather_words(1, 0, S)
        load_w1(2)
        w3_rows = w3.rearrange("(q t i) n -> t q i n", t=4, i=8)
        for t in range(4):
            nc.sync.dma_start(w3_raw[:, t, :], w3_rows[t])
        with nc.allow_non_contiguous_dma(reason="one bias value a partition"):
            nc.sync.dma_start(by_sb[:], by.rearrange("(n p) -> p n", p=P))
        nc.sync.dma_start(wgo_sb[:], wgo)
        gather_words(2, 0, HALF)
        gather_words(2, HALF, HALF)

        w1_codes = held([P, PASSES, H], U32, "w1_codes")
        w1_sc = held([P, PASSES, H], U8, "w1_sc")

        def prepare_w1(a, pieces):
            rounded = [held([P, H // 2, 4], BF16, "w1_bf%d_%d" % (a, u)) for u in range(2)]
            dst = [rounded[u][:].rearrange("p (t q i) j -> p t q i j", t=2, i=8) for u in range(2)]
            if a < PASSES - 1:
                src = w1_raw[a][:].rearrange("p j (q t i) -> p t q j i", t=4, i=8)
                for u in range(2):
                    nc.vector.tensor_copy(
                        rounded[u][:].rearrange("p (t q i) j -> p t q j i", t=2, i=8), src[:, 2 * u : 2 * u + 2]
                    )
            else:
                for pair in range(2):
                    src = w1_last[pair][:].rearrange("p j (q t i) -> p t q i j", t=4, i=8)
                    for u in range(2):
                        nc.vector.tensor_copy(dst[u][:, :, :, :, 2 * pair : 2 * pair + 2], src[:, 2 * u : 2 * u + 2])
            width = H // pieces
            for first in range(0, H, width):
                u, start = divmod(first, H // 2)
                cols = slice(first, first + width)
                nc.vector.quantize_mx(
                    w1_codes[:, a, cols].bitcast(FP8X4),
                    w1_sc[:, a, cols],
                    rounded[u][:, start : start + width, :].rearrange("p m j -> p (m j)"),
                )

        def product_pass(acc, g, a, stationary):
            half, start = divmod(g * CHUNK, HALF)
            for t in range(4):
                codes, scales = stationary(a, t)
                nc.tensor.matmul_mx(
                    acc[:, t, :],
                    lhsT=codes,
                    lhsT_scale=scales,
                    rhs=v_halves[a, half][:, start : start + CHUNK].bitcast(FP8X4),
                    rhs_scale=v_sc[a][:].bitcast(U8)[:, g * CHUNK : (g + 1) * CHUNK],
                    start=(a == 0 and t == 0),
                    stop=(a == PASSES - 1 and t == 3),
                )

        def w2_tile(a, t):
            return (
                w2_codes[:, a, 64 * t : 64 * (t + 1)].bitcast(U8).bitcast(FP4X4),
                w2_sc[:, a, 32 * t : 32 * (t + 1)].bitcast(U8),
            )

        def w1_tile(a, t):
            cols = slice(P * t, P * (t + 1))
            return w1_codes[:, a, cols].bitcast(FP8X4), w1_sc[:, a, cols]

        def products(chunks, banks, stationary, name):
            accs = {}
            for g in chunks:
                accs[g] = psum.tile([P, 4, CHUNK], F32, name=name, tag="bank%d" % banks[g])
            for a in range(PASSES):
                for g in chunks:
                    product_pass(accs[g], g, a, stationary)
            return accs

        damp = {g: held([P, CHUNK, 4], F32, "damp%d" % g) for g in range(CHUNKS) if g not in (2, 3)}
        sizes = {}
        roots = {}

        def magnitudes(b_ps, g):
            size = placed([P, 2, CHUNK, 4], F32, "b_abs%d" % g, ABS_AT[g // 2])
            for u in range(2):
                nc.scalar.activation(size[:, u], b_ps[g + u][:].rearrange("p t n -> p n t"), ACT.Abs)
                sizes[g + u] = size[:, u]

        def root_of(g):
            if g >= 4:
                roots[g] = placed([P, CHUNK, 4], F32, "root%d" % g, W3_AT + 2 * KIB * (g % 2))
            else:
                roots[g] = ring.tile([P, CHUNK, 4], F32, name="root")
            nc.scalar.activation(roots[g][:], sizes[g], ACT.Abs_reciprocal_sqrt, bias=warm_out[:])

        def square_of(g):
            nc.scalar.activation(damp[g][:], roots[g][:], ACT.Square)

        h_bf = {}
        h_codes = {}
        h_sc = [held([P, GROUP], U8, "h_sc%d" % group) for group in range(S // GROUP)]
        w3_codes = {}
        w3_sc = [held([P, P], U8, "w3_sc%d" % n) for n in range(N // P)]
        w3_bf = [placed([P, P, 4], BF16, "w3_bf%d" % n, ABS_AT[1] + n * KIB) for n in range(N // P)]
        a_sb = {g: held([P, CHUNK * 4], F32, "a_sb%d" % g) for g in range(4, CHUNKS)}

        def h_target(g, tag=None, spare=0):
            group, u = divmod(g, 2)
            if group not in h_bf:
                h_bf[group] = held([P, GROUP * (4 + spare)], BF16, "h_bf%d" % group, tag)
            return h_bf[group][:, u * CHUNK * 4 : (u + 1) * CHUNK * 4]

        def damped(a_ps, g):
            nc.vector.tensor_tensor(
                h_target(g).rearrange("p (n t) -> p n t", t=4),
                a_ps[g][:].rearrange("p t n -> p n t"),
                damp[g][:],
                ALU.mult,
            )

        def damped_aside(g, tag=None):
            nc.gpsimd.tensor_tensor(h_target(g, tag), a_sb[g][:], damp[g][:].rearrange("p n t -> p (n t)"), ALU.mult)

        def quantise_h(group, tag=None):
            h_codes[group] = held([P, GROUP], U32, "h_codes%d" % group, tag)
            nc.vector.quantize_mx(h_codes[group][:].bitcast(FP8X4), h_sc[group][:], h_bf[group][:, 0 : GROUP * 4])

        def prepare_w3(n, after):
            cols = slice(P * n, P * (n + 1))
            w3_codes[n] = held([P, P], U32, "w3_codes%d" % n, after)
            nc.scalar.copy(w3_bf[n][:], w3_raw[:, :, cols].rearrange("p t n -> p n t"))
            nc.vector.quantize_mx(
                w3_codes[n][:].bitcast(FP8X4), w3_sc[n][:], w3_bf[n][:].rearrange("p n t -> p (n t)")
            )

        def projection(group, n, bank, groups=1):
            y_ps = psum.tile([P, groups, GROUP], F32, name="y_ps", tag="bank%d" % bank)
            for u in range(groups):
                nc.tensor.matmul_mx(
                    y_ps[:, u, :],
                    lhsT=w3_codes[n][:].bitcast(FP8X4),
                    lhsT_scale=w3_sc[n][:],
                    rhs=h_codes[group + u][:].bitcast(FP8X4),
                    rhs_scale=h_sc[group + u][:],
                    start=True,
                    stop=True,
                )
            return y_ps[:].rearrange("p g n -> p (g n)")

        def places(group, n, groups=1):
            return cache[n][:].indirect(idx2[:, GROUP * group // 16 : GROUP * (group + groups) // 16])

        def weights(group, groups=1):
            return wgo_sb[:, GROUP * group : GROUP * (group + groups)]

        def biased(target, group, n, bank, groups=1):
            nc.scalar.activation(target, projection(group, n, bank, groups), ACT.Identity, bias=by_sb[:, n : n + 1])

        def scatter_product(group, n, y_sb, groups=1):
            nc.vector.tensor_tensor(places(group, n, groups), y_sb, weights(group, groups), ALU.mult)
            if group + groups == S // GROUP:
                nc.sync.dma_start(out[P * n : P * (n + 1), :], cache[n][:])

        def late_loads(pair):
            for g in (pair, pair + 1):
                b_ps.update(products([g], B_BANKS, w2_tile, "b_ps"))
            magnitudes(b_ps, pair)

        def late_factors(g):
            if g not in roots:
                root_of(g)
            a_ps.update(products([g], A_BANKS, w1_tile, "a_ps"))
            nc.scalar.copy(a_sb[g][:].rearrange("p (n t) -> p n t", t=4), a_ps[g][:].rearrange("p t n -> p n t"))
            square_of(g)

        b_ps = products(range(0, 4), B_BANKS, w2_tile, "b_ps")
        for g in (0, 2):
            magnitudes(b_ps, g)
            root_of(g)
            root_of(g + 1)
            if g == 0:
                square_of(g)
                square_of(g + 1)
        prepare_w1(0, 2)
        prepare_w1(1, 2)
        prepare_w1(2, 4)
        damp[2] = held([P, CHUNK, 4], F32, "damp2", "w1_bf2_0")
        nc.vector.tensor_tensor(damp[2][:], roots[2][:], roots[2][:], ALU.mult)
        damp[3] = held([P, CHUNK, 4], F32, "damp3", "w1_bf2_1")
        nc.gpsimd.tensor_tensor(damp[3][:], roots[3][:], roots[3][:], ALU.mult)
        a_ps = products(range(0, 4), A_BANKS, w1_tile, "a_ps")
        late_loads(4)
        damped(a_ps, 0)
        damped(a_ps, 1)
        prepare_w3(0, "damp0")
        quantise_h(0)
        y_first = projection(0, 0, 2)
        prepare_w3(1, "damp1")
        damped(a_ps, 2)
        damped(a_ps, 3)
        weighted_first = held([P, GROUP], F32, "weighted_first")
        nc.vector.scalar_tensor_tensor(weighted_first[:], y_first, by_sb[:, 0:1], weights(0), ALU.add, ALU.mult)
        prepare_w3(2, "w1_bf2_0")
        quantise_h(1)
        nc.vector.tensor_copy(places(0, 0), weighted_first[:])

        root_of(4)
        y_second = held([P, GROUP], F32, "y_second")
        biased(y_second[:], 0, 1, 3)
        weighted = held([P, 3, GROUP], F32, "weighted", "h_bf1")
        nc.gpsimd.tensor_tensor(weighted[:, 0, :], y_second[:], weights(0), ALU.mult)
        nc.vector.tensor_copy(places(0, 1), weighted[:, 0, :])
        late_factors(4)
        y_pair = held([P, 2, GROUP], F32, "y_pair", "stage")
        biased(y_pair[:, 0, :], 0, 2, 0)
        biased(y_pair[:, 1, :], 1, 0, 1)
        nc.gpsimd.tensor_tensor(
            weighted[:, 1:3, :].rearrange("p g n -> p (g n)"),
            y_pair[:].rearrange("p g n -> p (g n)"),
            weights(0, 2),
            ALU.mult,
        )
        nc.vector.tensor_copy(places(0, 2), weighted[:, 1, :])
        nc.vector.tensor_copy(places(1, 0), weighted[:, 2, :])
        damped_aside(4, "stage")
        late_factors(5)
        damped_aside(5)
        quantise_h(2)
        y_rest = held([P, 2, GROUP], F32, "y_rest")
        biased(y_rest[:, 0, :], 1, 1, 2)
        biased(y_rest[:, 1, :], 1, 2, 3)
        weighted_fifth = held([P, GROUP], F32, "weighted_fifth", "a_sb5")
        nc.gpsimd.tensor_tensor(weighted_fifth[:], y_rest[:, 0, :], weights(1), ALU.mult)
        nc.vector.tensor_copy(places(1, 1), weighted_fifth[:])
        h_target(6, "stage", spare=2)
        weighted_sixth = h_bf[3][:, GROUP * 4 :].bitcast(F32)
        nc.gpsimd.tensor_tensor(weighted_sixth, y_rest[:, 1, :], weights(1), ALU.mult)
        nc.vector.tensor_copy(places(1, 2), weighted_sixth)
        late_loads(6)
        late_factors(6)
        damped_aside(6)
        late_factors(7)
        y_third = h_bf[3][:, CHUNK * 4 : GROUP * 4].bitcast(F32)
        biased(y_third, 2, 0, 0)
        weighted_third = held([P, GROUP], F32, "weighted_third")
        nc.gpsimd.tensor_tensor(weighted_third[:], y_third, weights(2), ALU.mult)
        nc.vector.tensor_copy(places(2, 0), weighted_third[:])
        damped_aside(7)
        quantise_h(3)
        y_cover = held([P, GROUP], F32, "y_cover", "damp7")
        biased(y_cover[:], 2, 1, 1)
        scatter_product(2, 1, y_cover[:])
        for n in range(2):
            y_last = held([P, GROUP], F32, "y_last%d" % n)
            biased(y_last[:], 3, n, 2 + n)
            scatter_product(3, n, y_last[:])
        y_wide = held([P, HALF], F32, "y_wide")
        biased(y_wide[:], 2, 2, 6, groups=2)
        scatter_product(2, 2, y_wide[:], groups=2)
